import numpy as np
import ml_dtypes


def mxq(x, axis, fmt="e4m3"):
    dtype, down = {"e4m3": (ml_dtypes.float8_e4m3fn, 7), "e5m2": (ml_dtypes.float8_e5m2, 14)}[fmt]
    v = np.moveaxis(np.asarray(x, np.float32).astype(ml_dtypes.bfloat16).astype(np.float64), axis, -1)
    blocks = v.reshape(v.shape[:-1] + (-1, 32))
    amax = np.abs(blocks).max(-1, keepdims=True)
    byte = np.maximum(np.where(amax > 0, np.frexp(amax)[1] - 1 + 127, 0) - down, 1)
    scale = np.exp2(byte - 127.0)
    codes = (blocks / scale).astype(np.float32).astype(dtype).astype(np.float64)
    return np.moveaxis((codes * scale).reshape(v.shape), -1, axis)


WIDE = False


def mx_kscale(k):
    if not WIDE:
        return np.ones(k)
    levels = np.array([10, -10, 5, -5, 0])
    if k % 512:
        return np.exp2(np.random.permutation(np.resize(levels, k // 32))).repeat(32)
    a = np.empty((k // 512, 16))
    for p in range(k // 512):
        a[p, :8] = np.random.permutation(np.resize(levels, 8))
        for g in range(8):
            far = levels[np.abs(levels - a[p, g]) >= 10]
            a[p, g + 8] = far[np.random.randint(len(far))]
    return np.exp2(a.ravel()).repeat(32)


def f64(x):
    return np.asarray(x).astype(np.float64)


def striped(idx):
    return np.tile(np.asarray(idx).reshape(-1, 16).T, (8, 1)).astype(np.uint16)


def unstriped(offs):
    return offs[:16].T.reshape(-1).astype(np.int64)


E2M1 = np.array([0.0, 0.5, 1.0, 1.5, 2.0, 3.0, 4.0, 6.0, -0.0, -0.5, -1.0, -1.5, -2.0, -3.0, -4.0, -6.0])


def pack_weight(w, fmt):
    k, n = w.shape
    w = f64(np.asarray(w, np.float32).astype(ml_dtypes.bfloat16)).reshape(k // 32, 32, n)
    amax = np.abs(w).max(1)
    if fmt == "e4m3":
        byte = np.frexp(amax)[1] - 1 + 127 - 7
    else:
        mant, ex = np.frexp(amax / 6.0)
        byte = np.where(mant > 0.5, ex, ex - 1) + 127
    byte = np.clip(np.where(amax > 0, byte, 1), 1, 254)
    scaled = (w * np.exp2(127.0 - byte)[:, None, :]).reshape(k, n).astype(np.float32)
    by_word = np.ascontiguousarray(scaled.reshape(k // 512, 128, 4, n).transpose(0, 1, 3, 2))
    if fmt == "e4m3":
        words = by_word.astype(ml_dtypes.float8_e4m3fn).view(np.uint8)
    else:
        c = by_word.astype(ml_dtypes.float4_e2m1fn).view(np.uint8) & 0xF
        words = (c[..., 0::2] | (c[..., 1::2] << 4)).reshape(k // 512, 128, 2 * n)
    return np.ascontiguousarray(words), np.ascontiguousarray(byte.astype(np.uint8).reshape(k // 512, 16, n))


def unpack_weight(words, scales, fmt):
    g, _, n = scales.shape
    words = np.ascontiguousarray(words).reshape(g, 128, n, -1)
    if fmt == "e4m3":
        vals = words.view(ml_dtypes.float8_e4m3fn).astype(np.float64)
    else:
        nib = np.empty((g, 128, n, 4), np.uint8)
        nib[..., 0::2] = words & 0xF
        nib[..., 1::2] = words >> 4
        vals = E2M1[nib]
    vals = vals * np.repeat(np.exp2(scales.astype(np.float64) - 127.0), 8, axis=1)[..., None]
    return vals.transpose(0, 1, 3, 2).reshape(g * 512, n)


K, T, I, P, Q, G = 512, 4096, 1024, 512, 256, 64


def setup_inputs():
    n = np.random.standard_normal
    idx = (np.random.permutation(T // 16)[:I // 16, None] * 16 + np.arange(16)).reshape(-1)
    fk = mx_kscale(K)
    fp = mx_kscale(P)
    embp = pack_weight(n((K, T)) / fk[:, None], "e4m3")
    return {
        "emb_words": embp[0],
        "emb_scales": embp[1],
        "wp": (n((K, P)) * 1 / np.sqrt(K) * fk[:, None] / fp).astype(np.float32),
        "qt": (n((P, Q)) * 1.0 / np.sqrt(P) * fp[:, None]).astype(np.float32),
        "offs": striped(idx),
    }


def reference(emb_words, emb_scales, wp, qt, offs):
    idx = unstriped(offs)
    embu = unpack_weight(emb_words, emb_scales, "e4m3")
    wpq = mxq(f64(wp), 0, "e4m3")
    embidxg = embu[:, idx]
    dt = wpq.T @ embidxg
    qtq = mxq(f64(qt), 0, "e4m3")
    dtq = mxq(dt, 0, "e4m3")
    a = qtq.T @ dtq
    y = a.reshape(Q, G, I // G).max(axis=2)
    return y

@@ -1,0 +1,128 @@
+from contextlib import ExitStack
+
+import concourse.mybir as mybir
+
+K, T, I, PF, Q, G = 512, 4096, 1024, 512, 256, 64
+FLOPS = 2 * K * PF * I + 2 * PF * Q * I
+
+F32 = mybir.dt.float32
+BF16 = mybir.dt.bfloat16
+I32 = mybir.dt.int32
+U32 = mybir.dt.uint32
+U16 = mybir.dt.uint16
+U8 = mybir.dt.uint8
+FP8X4 = mybir.dt.float8_e4m3fn_x4
+
+P = 128
+PACK = 4
+RUN = I // G
+GATHER = 512
+CHUNK = 128
+STAGES = ((0, 2), (2, 2), (4, 2), (6, 1), (7, 1))
+
+
+def tile_attend_colbert_proj_kernel(tc, emb_words, emb_scales, wp, qt, offs, out):
+    nc = tc.nc
+    with ExitStack() as ctx:
+        keep = ctx.enter_context(tc.tile_pool(name="keep", bufs=1))
+        psum_d = ctx.enter_context(tc.psum_pool(name="psum_d", bufs=5))
+        psum_a = ctx.enter_context(tc.psum_pool(name="psum_a", bufs=3))
+
+        offsets = keep.tile([P, I // 16], U16, name="offsets")
+        pool_scales = keep.tile([P, T], U8, name="pool_scales", align_bytes=64)
+        pool_words = keep.tile([P, T], I32, name="pool_words", align_bytes=64)
+        w_raw = keep.tile([P, PACK, PF], F32, name="w_raw")
+        q_raw = keep.tile([P, PACK, Q], F32, name="q_raw")
+
+        nc.vector.memset(pool_scales[:].bitcast(I32), 0)
+        nc.sync.dma_start(out=w_raw[:], in_=wp.rearrange("(p j) c -> p j c", j=PACK))
+        nc.sync.dma_start(offsets[:], offs)
+        scale_rows = emb_scales[0].bitcast(I32)
+        for r in range(4):
+            nc.sync.dma_start(out=pool_scales[r:P:32, :].bitcast(I32), in_=scale_rows[r:16:4, :])
+        nc.sync.dma_start(out=pool_words[:], in_=emb_words[0].rearrange("p n t -> p (n t)").bitcast(I32))
+        nc.sync.dma_start(out=q_raw[:], in_=qt.rearrange("(p j) c -> p j c", j=PACK))
+
+        w_bf = keep.tile([P, PACK * PF], BF16, name="w_bf", align_bytes=64)
+        nc.scalar.copy(
+            out=w_bf[:].rearrange("p (t m j) -> p m j t", t=PACK, j=PACK),
+            in_=w_raw[:].rearrange("p j (m t) -> p m j t", t=PACK),
+        )
+        e_scales = keep.tile([P, I], U8, name="e_scales", align_bytes=64)
+        nc.vector.tensor_copy(e_scales[:], pool_scales[:].indirect(offsets[:]))
+        w_codes = keep.tile([P, PF], U32, name="w_codes", align_bytes=64)
+        w_scales = keep.tile([P, PF], U8, name="w_scales", align_bytes=64)
+        nc.vector.quantize_mx(out=w_codes[:].bitcast(FP8X4), scales=w_scales[:], in_=w_bf[:])
+
+        e_words = []
+        for u in range(I // GATHER):
+            words = keep.tile([P, GATHER], U32, name="e_words%d" % u, align_bytes=64)
+            cols = slice(u * GATHER // 16, (u + 1) * GATHER // 16)
+            nc.vector.tensor_copy(words[:], pool_words[:].bitcast(U32).indirect(offsets[:, cols]))
+            e_words.append(words)
+
+        q_bf = keep.tile([P, PACK * Q], BF16, name="q_bf", align_bytes=64)
+        q_dst = q_bf[:].rearrange("p (h c i j) -> p c j i h", h=2, i=2, j=PACK)
+        q_src = q_raw[:].rearrange("p j (c i h) -> p c j i h", i=2, h=2)
+        nc.scalar.copy(out=q_dst[:, 0:32], in_=q_src[:, 0:32])
+        nc.vector.tensor_copy(out=q_dst[:, 32:64], in_=q_src[:, 32:64])
+        q_codes = keep.tile([P, Q], U32, name="q_codes", align_bytes=64)
+        q_scales = keep.tile([P, Q], U8, name="q_scales", align_bytes=64)
+        nc.vector.quantize_mx(out=q_codes[:].bitcast(FP8X4), scales=q_scales[:], in_=q_bf[:])
+
+        best = keep.tile([P, 2, G], F32, name="best")
+
+        def project(first, count):
+            d_bf = keep.tile([P, count * CHUNK * PACK], BF16, name="d_bf%d" % first, align_bytes=64)
+            for c in range(count):
+                slot = (first + c) * CHUNK
+                words = e_words[slot // GATHER]
+                lo = slot % GATHER
+                bank = psum_d.tile([P, PACK, CHUNK], F32, name="d_bank")
+                for t in range(PACK):
+                    nc.tensor.matmul_mx(
+                        out=bank[:, t, :],
+                        lhsT=w_codes[:, t * P : (t + 1) * P].bitcast(FP8X4),
+                        lhsT_scale=w_scales[:, t * P : (t + 1) * P],
+                        rhs=words[:, lo : lo + CHUNK].bitcast(FP8X4),
+                        rhs_scale=e_scales[:, slot : slot + CHUNK],
+                        start=True,
+                        stop=True,
+                    )
+                nc.scalar.copy(
+                    out=d_bf[:, c * CHUNK * PACK : (c + 1) * CHUNK * PACK].rearrange("p (n t) -> p n t", t=PACK),
+                    in_=bank[:].rearrange("p t n -> p n t"),
+                )
+            return d_bf
+
+        def score(first, count, d_bf):
+            n = count * CHUNK
+            d_codes = keep.tile([P, n], U32, name="d_codes%d" % first, align_bytes=64)
+            d_scales = keep.tile([P, n], U8, name="d_scales%d" % first, align_bytes=64)
+            nc.vector.quantize_mx(out=d_codes[:].bitcast(FP8X4), scales=d_scales[:], in_=d_bf[:])
+            bank = psum_a.tile([P, 2, n], F32, name="a_bank")
+            for h in range(2):
+                nc.tensor.matmul_mx(
+                    out=bank[:, h, :],
+                    lhsT=q_codes[:, h * P : (h + 1) * P].bitcast(FP8X4),
+                    lhsT_scale=q_scales[:, h * P : (h + 1) * P],
+                    rhs=d_codes[:].bitcast(FP8X4),
+                    rhs_scale=d_scales[:],
+                    start=True,
+                    stop=True,
+                )
+            g0 = first * CHUNK // RUN
+            nc.vector.tensor_reduce(
+                out=best[:, :, g0 : g0 + n // RUN],
+                in_=bank[:].rearrange("p h (g s) -> p h g s", s=RUN),
+                axis=mybir.AxisListType.X,
+                op=mybir.AluOpType.max,
+            )
+
+        projected = [project(*STAGES[0]), project(*STAGES[1])]
+        for s, (first, count) in enumerate(STAGES):
+            if s + 2 < len(STAGES):
+                projected.append(project(*STAGES[s + 2]))
+            score(first, count, projected[s])
+
+        nc.sync.dma_start(out=out.rearrange("(m h) g -> m (h g)", h=2), in_=best[:].rearrange("p h g -> p (h g)"))

@@ -18,6 +18,7 @@ PACK = 4
 RUN = I // G
 GATHER = 512
 CHUNK = 128
+VECTOR_BANKS = (1,)
 STAGES = ((0, 2), (2, 2), (4, 2), (6, 1), (7, 1))
 
 
@@ -25,22 +26,23 @@ def tile_attend_colbert_proj_kernel(tc, emb_words, emb_scales, wp, qt, offs, out
     nc = tc.nc
     with ExitStack() as ctx:
         keep = ctx.enter_context(tc.tile_pool(name="keep", bufs=1))
-        psum_d = ctx.enter_context(tc.psum_pool(name="psum_d", bufs=5))
-        psum_a = ctx.enter_context(tc.psum_pool(name="psum_a", bufs=3))
+        psum_d = ctx.enter_context(tc.psum_pool(name="psum_d", bufs=4))
+        psum_a = ctx.enter_context(tc.psum_pool(name="psum_a", bufs=4))
 
         offsets = keep.tile([P, I // 16], U16, name="offsets")
-        pool_scales = keep.tile([P, T], U8, name="pool_scales", align_bytes=64)
+        pool_scales = keep.tile([P, T], U8, name="pool_scales", tag="scales", align_bytes=64)
         pool_words = keep.tile([P, T], I32, name="pool_words", align_bytes=64)
         w_raw = keep.tile([P, PACK, PF], F32, name="w_raw")
-        q_raw = keep.tile([P, PACK, Q], F32, name="q_raw")
+        q_raw = keep.tile([P, PACK, Q], F32, name="q_raw", tag="q_raw", align_bytes=64)
 
         nc.vector.memset(pool_scales[:].bitcast(I32), 0)
         nc.sync.dma_start(out=w_raw[:], in_=wp.rearrange("(p j) c -> p j c", j=PACK))
         nc.sync.dma_start(offsets[:], offs)
+        word_rows = emb_words[0].rearrange("p n t -> p (n t)").bitcast(I32)
         scale_rows = emb_scales[0].bitcast(I32)
         for r in range(4):
             nc.sync.dma_start(out=pool_scales[r:P:32, :].bitcast(I32), in_=scale_rows[r:16:4, :])
-        nc.sync.dma_start(out=pool_words[:], in_=emb_words[0].rearrange("p n t -> p (n t)").bitcast(I32))
+        nc.sync.dma_start(out=pool_words[:], in_=word_rows)
         nc.sync.dma_start(out=q_raw[:], in_=qt.rearrange("(p j) c -> p j c", j=PACK))
 
         w_bf = keep.tile([P, PACK * PF], BF16, name="w_bf", align_bytes=64)
@@ -51,8 +53,20 @@ def tile_attend_colbert_proj_kernel(tc, emb_words, emb_scales, wp, qt, offs, out
         e_scales = keep.tile([P, I], U8, name="e_scales", align_bytes=64)
         nc.vector.tensor_copy(e_scales[:], pool_scales[:].indirect(offsets[:]))
         w_codes = keep.tile([P, PF], U32, name="w_codes", align_bytes=64)
-        w_scales = keep.tile([P, PF], U8, name="w_scales", align_bytes=64)
+        w_scales = keep.tile([P, PF], U8, name="w_scales", tag="scales", align_bytes=64)
         nc.vector.quantize_mx(out=w_codes[:].bitcast(FP8X4), scales=w_scales[:], in_=w_bf[:])
+
+        warm = psum_a.tile([P, PF], F32, name="a_bank")
+        for r in range(3):
+            nc.tensor.matmul_mx(
+                out=warm[:],
+                lhsT=w_codes[:, :P].bitcast(FP8X4),
+                lhsT_scale=w_scales[:, :P],
+                rhs=w_codes[:].bitcast(FP8X4),
+                rhs_scale=w_scales[:],
+                start=True,
+                stop=True,
+            )
 
         e_words = []
         for u in range(I // GATHER):
@@ -64,16 +78,17 @@ def tile_attend_colbert_proj_kernel(tc, emb_words, emb_scales, wp, qt, offs, out
         q_bf = keep.tile([P, PACK * Q], BF16, name="q_bf", align_bytes=64)
         q_dst = q_bf[:].rearrange("p (h c i j) -> p c j i h", h=2, i=2, j=PACK)
         q_src = q_raw[:].rearrange("p j (c i h) -> p c j i h", i=2, h=2)
-        nc.scalar.copy(out=q_dst[:, 0:32], in_=q_src[:, 0:32])
-        nc.vector.tensor_copy(out=q_dst[:, 32:64], in_=q_src[:, 32:64])
+        nc.scalar.copy(out=q_dst, in_=q_src)
         q_codes = keep.tile([P, Q], U32, name="q_codes", align_bytes=64)
         q_scales = keep.tile([P, Q], U8, name="q_scales", align_bytes=64)
         nc.vector.quantize_mx(out=q_codes[:].bitcast(FP8X4), scales=q_scales[:], in_=q_bf[:])
 
         best = keep.tile([P, 2, G], F32, name="best")
 
+        d_all = keep.tile([P, I * PACK], BF16, name="d_all", tag="q_raw", align_bytes=64)
+
         def project(first, count):
-            d_bf = keep.tile([P, count * CHUNK * PACK], BF16, name="d_bf%d" % first, align_bytes=64)
+            d_bf = d_all[:, first * CHUNK * PACK : (first + count) * CHUNK * PACK]
             for c in range(count):
                 slot = (first + c) * CHUNK
                 words = e_words[slot // GATHER]
@@ -89,7 +104,8 @@ def tile_attend_colbert_proj_kernel(tc, emb_words, emb_scales, wp, qt, offs, out
                         start=True,
                         stop=True,
                     )
-                nc.scalar.copy(
+                copy = nc.vector.tensor_copy if first + c in VECTOR_BANKS else nc.scalar.copy
+                copy(
                     out=d_bf[:, c * CHUNK * PACK : (c + 1) * CHUNK * PACK].rearrange("p (n t) -> p n t", t=PACK),
                     in_=bank[:].rearrange("p t n -> p n t"),
                 )
@@ -99,7 +115,7 @@ def tile_attend_colbert_proj_kernel(tc, emb_words, emb_scales, wp, qt, offs, out
             n = count * CHUNK
             d_codes = keep.tile([P, n], U32, name="d_codes%d" % first, align_bytes=64)
             d_scales = keep.tile([P, n], U8, name="d_scales%d" % first, align_bytes=64)
-            nc.vector.quantize_mx(out=d_codes[:].bitcast(FP8X4), scales=d_scales[:], in_=d_bf[:])
+            nc.vector.quantize_mx(out=d_codes[:].bitcast(FP8X4), scales=d_scales[:], in_=d_bf)
             bank = psum_a.tile([P, 2, n], F32, name="a_bank")
             for h in range(2):
                 nc.tensor.matmul_mx(

@@ -56,18 +56,6 @@ def tile_attend_colbert_proj_kernel(tc, emb_words, emb_scales, wp, qt, offs, out
         w_scales = keep.tile([P, PF], U8, name="w_scales", tag="scales", align_bytes=64)
         nc.vector.quantize_mx(out=w_codes[:].bitcast(FP8X4), scales=w_scales[:], in_=w_bf[:])
 
-        warm = psum_a.tile([P, PF], F32, name="a_bank")
-        for r in range(3):
-            nc.tensor.matmul_mx(
-                out=warm[:],
-                lhsT=w_codes[:, :P].bitcast(FP8X4),
-                lhsT_scale=w_scales[:, :P],
-                rhs=w_codes[:].bitcast(FP8X4),
-                rhs_scale=w_scales[:],
-                start=True,
-                stop=True,
-            )
-
         e_words = []
         for u in range(I // GATHER):
             words = keep.tile([P, GATHER], U32, name="e_words%d" % u, align_bytes=64)

@@ -16,34 +16,43 @@ FP8X4 = mybir.dt.float8_e4m3fn_x4
 P = 128
 PACK = 4
 RUN = I // G
+LIST_ROWS = 16
+SCALE_ROWS = 16
+QUADRANT = 32
 GATHER = 512
 CHUNK = 128
-VECTOR_BANKS = (1,)
+VECTOR_CHUNK = 1
 STAGES = ((0, 2), (2, 2), (4, 2), (6, 1), (7, 1))
+BANKS = 4
 
 
 def tile_attend_colbert_proj_kernel(tc, emb_words, emb_scales, wp, qt, offs, out):
     nc = tc.nc
     with ExitStack() as ctx:
         keep = ctx.enter_context(tc.tile_pool(name="keep", bufs=1))
-        psum_d = ctx.enter_context(tc.psum_pool(name="psum_d", bufs=4))
-        psum_a = ctx.enter_context(tc.psum_pool(name="psum_a", bufs=4))
+        psum_d = ctx.enter_context(tc.psum_pool(name="psum_d", bufs=BANKS))
+        psum_a = ctx.enter_context(tc.psum_pool(name="psum_a", bufs=BANKS))
 
-        offsets = keep.tile([P, I // 16], U16, name="offsets")
+        offsets = keep.tile([P, I // LIST_ROWS], U16, name="offsets")
         pool_scales = keep.tile([P, T], U8, name="pool_scales", tag="scales", align_bytes=64)
         pool_words = keep.tile([P, T], I32, name="pool_words", align_bytes=64)
         w_raw = keep.tile([P, PACK, PF], F32, name="w_raw")
-        q_raw = keep.tile([P, PACK, Q], F32, name="q_raw", tag="q_raw", align_bytes=64)
+        q_raw = [
+            keep.tile([P, PACK, Q // 2], F32, name="q_raw%d" % u, tag="q_raw%d" % u, align_bytes=64) for u in range(2)
+        ]
 
         nc.vector.memset(pool_scales[:].bitcast(I32), 0)
+
         nc.sync.dma_start(out=w_raw[:], in_=wp.rearrange("(p j) c -> p j c", j=PACK))
         nc.sync.dma_start(offsets[:], offs)
         word_rows = emb_words[0].rearrange("p n t -> p (n t)").bitcast(I32)
         scale_rows = emb_scales[0].bitcast(I32)
         for r in range(4):
-            nc.sync.dma_start(out=pool_scales[r:P:32, :].bitcast(I32), in_=scale_rows[r:16:4, :])
+            nc.sync.dma_start(out=pool_scales[r:P:QUADRANT, :].bitcast(I32), in_=scale_rows[r:SCALE_ROWS:4, :])
         nc.sync.dma_start(out=pool_words[:], in_=word_rows)
-        nc.sync.dma_start(out=q_raw[:], in_=qt.rearrange("(p j) c -> p j c", j=PACK))
+        q_rows = qt.rearrange("(p j) c -> p j c", j=PACK)
+        for u in range(2):
+            nc.sync.dma_start(out=q_raw[u][:], in_=q_rows[:, :, u * Q // 2 : (u + 1) * Q // 2])
 
         w_bf = keep.tile([P, PACK * PF], BF16, name="w_bf", align_bytes=64)
         nc.scalar.copy(
@@ -59,21 +68,22 @@ def tile_attend_colbert_proj_kernel(tc, emb_words, emb_scales, wp, qt, offs, out
         e_words = []
         for u in range(I // GATHER):
             words = keep.tile([P, GATHER], U32, name="e_words%d" % u, align_bytes=64)
-            cols = slice(u * GATHER // 16, (u + 1) * GATHER // 16)
+            cols = slice(u * GATHER // LIST_ROWS, (u + 1) * GATHER // LIST_ROWS)
             nc.vector.tensor_copy(words[:], pool_words[:].bitcast(U32).indirect(offsets[:, cols]))
             e_words.append(words)
 
         q_bf = keep.tile([P, PACK * Q], BF16, name="q_bf", align_bytes=64)
         q_dst = q_bf[:].rearrange("p (h c i j) -> p c j i h", h=2, i=2, j=PACK)
-        q_src = q_raw[:].rearrange("p j (c i h) -> p c j i h", i=2, h=2)
-        nc.scalar.copy(out=q_dst, in_=q_src)
+        for u in range(2):
+            q_src = q_raw[u][:].rearrange("p j (c i h) -> p c j i h", i=2, h=2)
+            nc.scalar.copy(out=q_dst[:, 32 * u : 32 * (u + 1)], in_=q_src)
         q_codes = keep.tile([P, Q], U32, name="q_codes", align_bytes=64)
         q_scales = keep.tile([P, Q], U8, name="q_scales", align_bytes=64)
         nc.vector.quantize_mx(out=q_codes[:].bitcast(FP8X4), scales=q_scales[:], in_=q_bf[:])
 
         best = keep.tile([P, 2, G], F32, name="best")
 
-        d_all = keep.tile([P, I * PACK], BF16, name="d_all", tag="q_raw", align_bytes=64)
+        d_all = keep.tile([P, I * PACK], BF16, name="d_all", tag="q_raw1", align_bytes=64)
 
         def project(first, count):
             d_bf = d_all[:, first * CHUNK * PACK : (first + count) * CHUNK * PACK]
@@ -92,7 +102,7 @@ def tile_attend_colbert_proj_kernel(tc, emb_words, emb_scales, wp, qt, offs, out
                         start=True,
                         stop=True,
                     )
-                copy = nc.vector.tensor_copy if first + c in VECTOR_BANKS else nc.scalar.copy
+                copy = nc.vector.tensor_copy if first + c == VECTOR_CHUNK else nc.scalar.copy
                 copy(
                     out=d_bf[:, c * CHUNK * PACK : (c + 1) * CHUNK * PACK].rearrange("p (n t) -> p n t", t=PACK),
                     in_=bank[:].rearrange("p t n -> p n t"),

@@ -19,6 +19,7 @@ RUN = I // G
 LIST_ROWS = 16
 SCALE_ROWS = 16
 QUADRANT = 32
+SPREAD = P // SCALE_ROWS
 GATHER = 512
 CHUNK = 128
 VECTOR_CHUNK = 1
@@ -42,13 +43,14 @@ def tile_attend_colbert_proj_kernel(tc, emb_words, emb_scales, wp, qt, offs, out
         ]
 
         nc.vector.memset(pool_scales[:].bitcast(I32), 0)
+        e_scales = keep.tile([P, I], U8, name="e_scales", align_bytes=64)
+        nc.vector.memset(e_scales[:].bitcast(I32), 0)
 
         nc.sync.dma_start(out=w_raw[:], in_=wp.rearrange("(p j) c -> p j c", j=PACK))
         nc.sync.dma_start(offsets[:], offs)
         word_rows = emb_words[0].rearrange("p n t -> p (n t)").bitcast(I32)
         scale_rows = emb_scales[0].bitcast(I32)
-        for r in range(4):
-            nc.sync.dma_start(out=pool_scales[r:P:QUADRANT, :].bitcast(I32), in_=scale_rows[r:SCALE_ROWS:4, :])
+        nc.sync.dma_start(out=pool_scales[SPREAD // 2 : P : SPREAD, :].bitcast(I32), in_=scale_rows)
         nc.sync.dma_start(out=pool_words[:], in_=word_rows)
         q_rows = qt.rearrange("(p j) c -> p j c", j=PACK)
         for u in range(2):
@@ -59,8 +61,13 @@ def tile_attend_colbert_proj_kernel(tc, emb_words, emb_scales, wp, qt, offs, out
             out=w_bf[:].rearrange("p (t m j) -> p m j t", t=PACK, j=PACK),
             in_=w_raw[:].rearrange("p j (m t) -> p m j t", t=PACK),
         )
-        e_scales = keep.tile([P, I], U8, name="e_scales", align_bytes=64)
-        nc.vector.tensor_copy(e_scales[:], pool_scales[:].indirect(offsets[:]))
+        e_spread = keep.tile([P, I], U8, name="e_spread", align_bytes=64)
+        nc.vector.tensor_copy(e_spread[:], pool_scales[:].indirect(offsets[:]))
+        for r in range(4):
+            nc.scalar.dma_start(
+                out=e_scales[r:P:QUADRANT, :].bitcast(I32),
+                in_=e_spread[SPREAD * r + SPREAD // 2 : P : QUADRANT, :].bitcast(I32),
+            )
         w_codes = keep.tile([P, PF], U32, name="w_codes", align_bytes=64)
         w_scales = keep.tile([P, PF], U8, name="w_scales", tag="scales", align_bytes=64)
         nc.vector.quantize_mx(out=w_codes[:].bitcast(FP8X4), scales=w_scales[:], in_=w_bf[:])

@@ -19,58 +19,48 @@ RUN = I // G
 LIST_ROWS = 16
 SCALE_ROWS = 16
 QUADRANT = 32
-SPREAD = P // SCALE_ROWS
 GATHER = 512
-CHUNK = 128
-VECTOR_CHUNK = 1
+TOP = P - SCALE_ROWS
+CHUNKS = ((0, 128, "v"), (128, 128, "s"), (256, 128, "s"), (384, 128, "s"), (512, 128, "v"), (640, 128, "s"), (768, 128, "s"), (896, 128, "s"))
 STAGES = ((0, 2), (2, 2), (4, 2), (6, 1), (7, 1))
-BANKS = 4
+D_BANKS, A_BANKS = 4, 4
+W_SPLIT = 104
+LAG = 2
+AHEAD = 2
 
 
 def tile_attend_colbert_proj_kernel(tc, emb_words, emb_scales, wp, qt, offs, out):
     nc = tc.nc
     with ExitStack() as ctx:
         keep = ctx.enter_context(tc.tile_pool(name="keep", bufs=1))
-        psum_d = ctx.enter_context(tc.psum_pool(name="psum_d", bufs=BANKS))
-        psum_a = ctx.enter_context(tc.psum_pool(name="psum_a", bufs=BANKS))
+        psum_d = ctx.enter_context(tc.psum_pool(name="psum_d", bufs=D_BANKS))
+        psum_a = ctx.enter_context(tc.psum_pool(name="psum_a", bufs=A_BANKS))
 
         offsets = keep.tile([P, I // LIST_ROWS], U16, name="offsets")
-        pool_scales = keep.tile([P, T], U8, name="pool_scales", tag="scales", align_bytes=64)
+        pool_scales = keep.tile([P, T], U8, name="pool_scales", align_bytes=64)
         pool_words = keep.tile([P, T], I32, name="pool_words", align_bytes=64)
-        w_raw = keep.tile([P, PACK, PF], F32, name="w_raw")
-        q_raw = [
-            keep.tile([P, PACK, Q // 2], F32, name="q_raw%d" % u, tag="q_raw%d" % u, align_bytes=64) for u in range(2)
-        ]
-
-        nc.vector.memset(pool_scales[:].bitcast(I32), 0)
+        w_raw = [keep.tile([P, PACK, PF // 2], F32, name="w_raw%d" % u) for u in range(2)]
+        q_raw = [keep.tile([P, PACK, Q // 2], F32, name="q_raw%d" % u, align_bytes=64) for u in range(2)]
         e_scales = keep.tile([P, I], U8, name="e_scales", align_bytes=64)
+
+        nc.vector.memset(pool_scales[:TOP, :].bitcast(I32), 0)
         nc.vector.memset(e_scales[:].bitcast(I32), 0)
 
-        nc.sync.dma_start(out=w_raw[:], in_=wp.rearrange("(p j) c -> p j c", j=PACK))
-        nc.sync.dma_start(offsets[:], offs)
         word_rows = emb_words[0].rearrange("p n t -> p (n t)").bitcast(I32)
-        scale_rows = emb_scales[0].bitcast(I32)
-        nc.sync.dma_start(out=pool_scales[SPREAD // 2 : P : SPREAD, :].bitcast(I32), in_=scale_rows)
+        nc.sync.dma_start(out=pool_scales[TOP:, :].bitcast(I32), in_=emb_scales[0].bitcast(I32))
+        nc.sync.dma_start(offsets[:], offs)
         nc.sync.dma_start(out=pool_words[:], in_=word_rows)
+        w_rows = wp.rearrange("(p j) c -> p j c", j=PACK)
+        for u in range(2):
+            nc.sync.dma_start(out=w_raw[u][:], in_=w_rows[:, :, u * PF // 2 : (u + 1) * PF // 2])
         q_rows = qt.rearrange("(p j) c -> p j c", j=PACK)
         for u in range(2):
             nc.sync.dma_start(out=q_raw[u][:], in_=q_rows[:, :, u * Q // 2 : (u + 1) * Q // 2])
 
-        w_bf = keep.tile([P, PACK * PF], BF16, name="w_bf", align_bytes=64)
-        nc.scalar.copy(
-            out=w_bf[:].rearrange("p (t m j) -> p m j t", t=PACK, j=PACK),
-            in_=w_raw[:].rearrange("p j (m t) -> p m j t", t=PACK),
-        )
-        e_spread = keep.tile([P, I], U8, name="e_spread", align_bytes=64)
-        nc.vector.tensor_copy(e_spread[:], pool_scales[:].indirect(offsets[:]))
+        e_top = keep.tile([P, I], U8, name="e_top", align_bytes=64)
+        nc.vector.tensor_copy(e_top[:], pool_scales[:].indirect(offsets[:]))
         for r in range(4):
-            nc.scalar.dma_start(
-                out=e_scales[r:P:QUADRANT, :].bitcast(I32),
-                in_=e_spread[SPREAD * r + SPREAD // 2 : P : QUADRANT, :].bitcast(I32),
-            )
-        w_codes = keep.tile([P, PF], U32, name="w_codes", align_bytes=64)
-        w_scales = keep.tile([P, PF], U8, name="w_scales", tag="scales", align_bytes=64)
-        nc.vector.quantize_mx(out=w_codes[:].bitcast(FP8X4), scales=w_scales[:], in_=w_bf[:])
+            nc.scalar.dma_start(out=e_scales[r:P:QUADRANT, :].bitcast(I32), in_=e_top[TOP + r : P : 4, :].bitcast(I32))
 
         e_words = []
         for u in range(I // GATHER):
@@ -78,6 +68,34 @@ def tile_attend_colbert_proj_kernel(tc, emb_words, emb_scales, wp, qt, offs, out
             cols = slice(u * GATHER // LIST_ROWS, (u + 1) * GATHER // LIST_ROWS)
             nc.vector.tensor_copy(words[:], pool_words[:].bitcast(U32).indirect(offsets[:, cols]))
             e_words.append(words)
+
+        for u in range(3):
+            idle = psum_a.tile([P, GATHER], F32, name="a_bank")
+            nc.tensor.matmul_mx(
+                out=idle[:],
+                lhsT=e_words[0][:, :P].bitcast(FP8X4),
+                lhsT_scale=e_top[:, :P],
+                rhs=e_words[0][:].bitcast(FP8X4),
+                rhs_scale=e_top[:, :GATHER],
+                start=True,
+                stop=True,
+            )
+
+        w_bf = keep.tile([P, PACK * PF], BF16, name="w_bf", align_bytes=64)
+        w_dst = w_bf[:].rearrange("p (t m j) -> p m j t", t=PACK, j=PACK)
+        w_src = [w[:].rearrange("p j (m t) -> p m j t", t=PACK) for w in w_raw]
+        half = P // 2
+        nc.scalar.copy(out=w_dst[:, :half], in_=w_src[0])
+        nc.vector.tensor_copy(out=w_dst[:, half:W_SPLIT], in_=w_src[1][:, : W_SPLIT - half])
+        nc.scalar.copy(out=w_dst[:, W_SPLIT:], in_=w_src[1][:, W_SPLIT - half :])
+        w_codes = keep.tile([P, PF], U32, name="w_codes", align_bytes=64)
+        w_scales = keep.tile([P, PF], U8, name="w_scales", align_bytes=64)
+        for t in range(PACK):
+            nc.vector.quantize_mx(
+                out=w_codes[:, t * P : (t + 1) * P].bitcast(FP8X4),
+                scales=w_scales[:, t * P : (t + 1) * P],
+                in_=w_bf[:, t * PF : (t + 1) * PF],
+            )
 
         q_bf = keep.tile([P, PACK * Q], BF16, name="q_bf", align_bytes=64)
         q_dst = q_bf[:].rearrange("p (h c i j) -> p c j i h", h=2, i=2, j=PACK)
@@ -89,38 +107,37 @@ def tile_attend_colbert_proj_kernel(tc, emb_words, emb_scales, wp, qt, offs, out
         nc.vector.quantize_mx(out=q_codes[:].bitcast(FP8X4), scales=q_scales[:], in_=q_bf[:])
 
         best = keep.tile([P, 2, G], F32, name="best")
-
-        d_all = keep.tile([P, I * PACK], BF16, name="d_all", tag="q_raw1", align_bytes=64)
+        d_all = keep.tile([P, I * PACK], BF16, name="d_all", align_bytes=64)
 
         def project(first, count):
-            d_bf = d_all[:, first * CHUNK * PACK : (first + count) * CHUNK * PACK]
-            for c in range(count):
-                slot = (first + c) * CHUNK
+            for slot, n, engine in CHUNKS[first : first + count]:
                 words = e_words[slot // GATHER]
                 lo = slot % GATHER
-                bank = psum_d.tile([P, PACK, CHUNK], F32, name="d_bank")
+                bank = psum_d.tile([P, PACK, n], F32, name="d_bank")
                 for t in range(PACK):
                     nc.tensor.matmul_mx(
                         out=bank[:, t, :],
                         lhsT=w_codes[:, t * P : (t + 1) * P].bitcast(FP8X4),
                         lhsT_scale=w_scales[:, t * P : (t + 1) * P],
-                        rhs=words[:, lo : lo + CHUNK].bitcast(FP8X4),
-                        rhs_scale=e_scales[:, slot : slot + CHUNK],
+                        rhs=words[:, lo : lo + n].bitcast(FP8X4),
+                        rhs_scale=e_scales[:, slot : slot + n],
                         start=True,
                         stop=True,
                     )
-                copy = nc.vector.tensor_copy if first + c == VECTOR_CHUNK else nc.scalar.copy
+                copy = nc.vector.tensor_copy if engine == "v" else nc.scalar.copy
                 copy(
-                    out=d_bf[:, c * CHUNK * PACK : (c + 1) * CHUNK * PACK].rearrange("p (n t) -> p n t", t=PACK),
+                    out=d_all[:, slot * PACK : (slot + n) * PACK].rearrange("p (n t) -> p n t", t=PACK),
                     in_=bank[:].rearrange("p t n -> p n t"),
                 )
-            return d_bf
 
-        def score(first, count, d_bf):
-            n = count * CHUNK
+        def score(first, count):
+            slot = CHUNKS[first][0]
+            n = sum(c[1] for c in CHUNKS[first : first + count])
             d_codes = keep.tile([P, n], U32, name="d_codes%d" % first, align_bytes=64)
             d_scales = keep.tile([P, n], U8, name="d_scales%d" % first, align_bytes=64)
-            nc.vector.quantize_mx(out=d_codes[:].bitcast(FP8X4), scales=d_scales[:], in_=d_bf)
+            nc.vector.quantize_mx(
+                out=d_codes[:].bitcast(FP8X4), scales=d_scales[:], in_=d_all[:, slot * PACK : (slot + n) * PACK]
+            )
             bank = psum_a.tile([P, 2, n], F32, name="a_bank")
             for h in range(2):
                 nc.tensor.matmul_mx(
@@ -132,7 +149,10 @@ def tile_attend_colbert_proj_kernel(tc, emb_words, emb_scales, wp, qt, offs, out
                     start=True,
                     stop=True,
                 )
-            g0 = first * CHUNK // RUN
+            return bank, slot, n
+
+        def reduce(bank, slot, n):
+            g0 = slot // RUN
             nc.vector.tensor_reduce(
                 out=best[:, :, g0 : g0 + n // RUN],
                 in_=bank[:].rearrange("p h (g s) -> p h g s", s=RUN),
@@ -140,10 +160,16 @@ def tile_attend_colbert_proj_kernel(tc, emb_words, emb_scales, wp, qt, offs, out
                 op=mybir.AluOpType.max,
             )
 
-        projected = [project(*STAGES[0]), project(*STAGES[1])]
-        for s, (first, count) in enumerate(STAGES):
-            if s + 2 < len(STAGES):
-                projected.append(project(*STAGES[s + 2]))
-            score(first, count, projected[s])
+        scored = []
+        for s in range(AHEAD):
+            project(*STAGES[s])
+        for s, stage in enumerate(STAGES):
+            if s + AHEAD < len(STAGES):
+                project(*STAGES[s + AHEAD])
+            scored.append(score(*stage))
+            if s >= LAG:
+                reduce(*scored[s - LAG])
+        for late in scored[len(STAGES) - LAG :]:
+            reduce(*late)
 
         nc.sync.dma_start(out=out.rearrange("(m h) g -> m (h g)", h=2), in_=best[:].rearrange("p h g -> p (h g)"))

@@ -21,7 +21,7 @@ SCALE_ROWS = 16
 QUADRANT = 32
 GATHER = 512
 TOP = P - SCALE_ROWS
-CHUNKS = ((0, 128, "v"), (128, 128, "s"), (256, 128, "s"), (384, 128, "s"), (512, 128, "v"), (640, 128, "s"), (768, 128, "s"), (896, 128, "s"))
+CHUNKS = ((0, 128, "s"), (128, 128, "v"), (256, 128, "s"), (384, 128, "s"), (512, 128, "v"), (640, 128, "s"), (768, 128, "s"), (896, 128, "s"))
 STAGES = ((0, 2), (2, 2), (4, 2), (6, 1), (7, 1))
 D_BANKS, A_BANKS = 4, 4
 W_SPLIT = 104
@@ -37,10 +37,9 @@ def tile_attend_colbert_proj_kernel(tc, emb_words, emb_scales, wp, qt, offs, out
         psum_a = ctx.enter_context(tc.psum_pool(name="psum_a", bufs=A_BANKS))
 
         offsets = keep.tile([P, I // LIST_ROWS], U16, name="offsets")
-        pool_scales = keep.tile([P, T], U8, name="pool_scales", align_bytes=64)
+        pool_scales = keep.tile([P, T], U8, name="pool_scales", tag="scales", align_bytes=64)
         pool_words = keep.tile([P, T], I32, name="pool_words", align_bytes=64)
         w_raw = [keep.tile([P, PACK, PF // 2], F32, name="w_raw%d" % u) for u in range(2)]
-        q_raw = [keep.tile([P, PACK, Q // 2], F32, name="q_raw%d" % u, align_bytes=64) for u in range(2)]
         e_scales = keep.tile([P, I], U8, name="e_scales", align_bytes=64)
 
         nc.vector.memset(pool_scales[:TOP, :].bitcast(I32), 0)
@@ -53,14 +52,18 @@ def tile_attend_colbert_proj_kernel(tc, emb_words, emb_scales, wp, qt, offs, out
         w_rows = wp.rearrange("(p j) c -> p j c", j=PACK)
         for u in range(2):
             nc.sync.dma_start(out=w_raw[u][:], in_=w_rows[:, :, u * PF // 2 : (u + 1) * PF // 2])
-        q_rows = qt.rearrange("(p j) c -> p j c", j=PACK)
-        for u in range(2):
-            nc.sync.dma_start(out=q_raw[u][:], in_=q_rows[:, :, u * Q // 2 : (u + 1) * Q // 2])
 
         e_top = keep.tile([P, I], U8, name="e_top", align_bytes=64)
         nc.vector.tensor_copy(e_top[:], pool_scales[:].indirect(offsets[:]))
         for r in range(4):
-            nc.scalar.dma_start(out=e_scales[r:P:QUADRANT, :].bitcast(I32), in_=e_top[TOP + r : P : 4, :].bitcast(I32))
+            nc.sync.dma_start(out=e_scales[r:P:QUADRANT, :].bitcast(I32), in_=e_top[TOP + r : P : 4, :].bitcast(I32))
+        held = keep.tile([P, PACK * Q], F32, name="held", tag="scales", align_bytes=64)
+        q_rows = qt.rearrange("(p j) c -> p j c", j=PACK)
+        q_raw = []
+        for u in range(2):
+            lo = PACK * u * Q // 2
+            q_raw.append(held[:, lo : lo + PACK * Q // 2].rearrange("p (j c) -> p j c", j=PACK))
+            nc.sync.dma_start(out=q_raw[u], in_=q_rows[:, :, u * Q // 2 : (u + 1) * Q // 2])
 
         e_words = []
         for u in range(I // GATHER):
@@ -107,7 +110,7 @@ def tile_attend_colbert_proj_kernel(tc, emb_words, emb_scales, wp, qt, offs, out
         nc.vector.quantize_mx(out=q_codes[:].bitcast(FP8X4), scales=q_scales[:], in_=q_bf[:])
 
         best = keep.tile([P, 2, G], F32, name="best")
-        d_all = keep.tile([P, I * PACK], BF16, name="d_all", align_bytes=64)
+        d_all = keep.tile([P, I * PACK], BF16, name="d_all", tag="scales", align_bytes=64)
 
         def project(first, count):
             for slot, n, engine in CHUNKS[first : first + count]:

@@ -42,13 +42,14 @@ def tile_attend_colbert_proj_kernel(tc, emb_words, emb_scales, wp, qt, offs, out
         w_raw = [keep.tile([P, PACK, PF // 2], F32, name="w_raw%d" % u) for u in range(2)]
         e_scales = keep.tile([P, I], U8, name="e_scales", align_bytes=64)
 
-        nc.vector.memset(pool_scales[:TOP, :].bitcast(I32), 0)
+        nc.vector.memset(pool_scales[:].bitcast(I32), 0)
         nc.vector.memset(e_scales[:].bitcast(I32), 0)
 
         word_rows = emb_words[0].rearrange("p n t -> p (n t)").bitcast(I32)
-        nc.sync.dma_start(out=pool_scales[TOP:, :].bitcast(I32), in_=emb_scales[0].bitcast(I32))
         nc.sync.dma_start(offsets[:], offs)
-        nc.sync.dma_start(out=pool_words[:], in_=word_rows)
+        nc.sync.dma_start(out=pool_words[:, :1024], in_=word_rows[:, :1024])
+        nc.sync.dma_start(out=pool_scales[4:P:8, :].bitcast(I32), in_=emb_scales[0].bitcast(I32))
+        nc.sync.dma_start(out=pool_words[:, 1024:], in_=word_rows[:, 1024:])
         w_rows = wp.rearrange("(p j) c -> p j c", j=PACK)
         for u in range(2):
             nc.sync.dma_start(out=w_raw[u][:], in_=w_rows[:, :, u * PF // 2 : (u + 1) * PF // 2])
@@ -56,7 +57,7 @@ def tile_attend_colbert_proj_kernel(tc, emb_words, emb_scales, wp, qt, offs, out
         e_top = keep.tile([P, I], U8, name="e_top", align_bytes=64)
         nc.vector.tensor_copy(e_top[:], pool_scales[:].indirect(offsets[:]))
         for r in range(4):
-            nc.sync.dma_start(out=e_scales[r:P:QUADRANT, :].bitcast(I32), in_=e_top[TOP + r : P : 4, :].bitcast(I32))
+            nc.sync.dma_start(out=e_scales[r:P:QUADRANT, :].bitcast(I32), in_=e_top[8 * r + 4 : P : QUADRANT, :].bitcast(I32))
         held = keep.tile([P, PACK * Q], F32, name="held", tag="scales", align_bytes=64)
         q_rows = qt.rearrange("(p j) c -> p j c", j=PACK)
         q_raw = []

@@ -17,16 +17,15 @@ P = 128
 PACK = 4
 RUN = I // G
 LIST_ROWS = 16
-SCALE_ROWS = 16
 QUADRANT = 32
 GATHER = 512
-TOP = P - SCALE_ROWS
-CHUNKS = ((0, 128, "s"), (128, 128, "v"), (256, 128, "s"), (384, 128, "s"), (512, 128, "v"), (640, 128, "s"), (768, 128, "s"), (896, 128, "s"))
-STAGES = ((0, 2), (2, 2), (4, 2), (6, 1), (7, 1))
+CHUNK = 128
+VECTOR_CHUNKS = (3,)
+STAGES = (1, 1, 2, 2, 1, 1)
 D_BANKS, A_BANKS = 4, 4
-W_SPLIT = 104
-LAG = 2
+LAG = 3
 AHEAD = 2
+WARM_PASSES, WARM_COLUMNS = 4, 64
 
 
 def tile_attend_colbert_proj_kernel(tc, emb_words, emb_scales, wp, qt, offs, out):
@@ -37,34 +36,50 @@ def tile_attend_colbert_proj_kernel(tc, emb_words, emb_scales, wp, qt, offs, out
         psum_a = ctx.enter_context(tc.psum_pool(name="psum_a", bufs=A_BANKS))
 
         offsets = keep.tile([P, I // LIST_ROWS], U16, name="offsets")
-        pool_scales = keep.tile([P, T], U8, name="pool_scales", tag="scales", align_bytes=64)
+        pool_scales = keep.tile([P, T], U8, name="pool_scales", align_bytes=64)
         pool_words = keep.tile([P, T], I32, name="pool_words", align_bytes=64)
-        w_raw = [keep.tile([P, PACK, PF // 2], F32, name="w_raw%d" % u) for u in range(2)]
+        w_raw = keep.tile([P, PACK, PF], F32, name="w_raw")
+        q_raw = [keep.tile([P, PACK, Q // 2], F32, name="q_raw%d" % u) for u in range(2)]
         e_scales = keep.tile([P, I], U8, name="e_scales", align_bytes=64)
 
         nc.vector.memset(pool_scales[:].bitcast(I32), 0)
         nc.vector.memset(e_scales[:].bitcast(I32), 0)
 
-        word_rows = emb_words[0].rearrange("p n t -> p (n t)").bitcast(I32)
+        nc.sync.dma_start(out=w_raw[:], in_=wp.rearrange("(p j) c -> p j c", j=PACK))
         nc.sync.dma_start(offsets[:], offs)
-        nc.sync.dma_start(out=pool_words[:, :1024], in_=word_rows[:, :1024])
-        nc.sync.dma_start(out=pool_scales[4:P:8, :].bitcast(I32), in_=emb_scales[0].bitcast(I32))
-        nc.sync.dma_start(out=pool_words[:, 1024:], in_=word_rows[:, 1024:])
-        w_rows = wp.rearrange("(p j) c -> p j c", j=PACK)
-        for u in range(2):
-            nc.sync.dma_start(out=w_raw[u][:], in_=w_rows[:, :, u * PF // 2 : (u + 1) * PF // 2])
+        nc.sync.dma_start(out=pool_scales[32:96:4, :].bitcast(I32), in_=emb_scales[0].bitcast(I32))
+        nc.sync.dma_start(out=pool_words[:], in_=emb_words[0].rearrange("p n t -> p (n t)").bitcast(I32))
 
-        e_top = keep.tile([P, I], U8, name="e_top", align_bytes=64)
-        nc.vector.tensor_copy(e_top[:], pool_scales[:].indirect(offsets[:]))
+        e_spread = keep.tile([P, I], U8, name="e_spread", align_bytes=64)
+        nc.vector.tensor_copy(e_spread[:], pool_scales[:].indirect(offsets[:]))
         for r in range(4):
-            nc.sync.dma_start(out=e_scales[r:P:QUADRANT, :].bitcast(I32), in_=e_top[8 * r + 4 : P : QUADRANT, :].bitcast(I32))
-        held = keep.tile([P, PACK * Q], F32, name="held", tag="scales", align_bytes=64)
+            nc.sync.dma_start(
+                out=e_scales[r:P:QUADRANT, :].bitcast(I32), in_=e_spread[32 + 4 * r : 96 : 16, :].bitcast(I32)
+            )
         q_rows = qt.rearrange("(p j) c -> p j c", j=PACK)
-        q_raw = []
         for u in range(2):
-            lo = PACK * u * Q // 2
-            q_raw.append(held[:, lo : lo + PACK * Q // 2].rearrange("p (j c) -> p j c", j=PACK))
-            nc.sync.dma_start(out=q_raw[u], in_=q_rows[:, :, u * Q // 2 : (u + 1) * Q // 2])
+            nc.sync.dma_start(out=q_raw[u][:], in_=q_rows[:, :, u * Q // 2 : (u + 1) * Q // 2])
+
+        w_bf = keep.tile([P, PACK * PF], BF16, name="w_bf", align_bytes=64)
+        nc.scalar.copy(
+            out=w_bf[:].rearrange("p (t m j) -> p m j t", t=PACK, j=PACK),
+            in_=w_raw[:].rearrange("p j (m t) -> p m j t", t=PACK),
+        )
+        w_codes = keep.tile([P, PF], U32, name="w_codes", align_bytes=64)
+        w_scales = keep.tile([P, PF], U8, name="w_scales", align_bytes=64)
+        nc.vector.quantize_mx(out=w_codes[:].bitcast(FP8X4), scales=w_scales[:], in_=w_bf[:])
+
+        for u in range(WARM_PASSES):
+            idle = psum_a.tile([P, PF], F32, name="a_bank")
+            nc.tensor.matmul_mx(
+                out=idle[:WARM_COLUMNS, :],
+                lhsT=w_codes[:, :WARM_COLUMNS].bitcast(FP8X4),
+                lhsT_scale=w_scales[:, :WARM_COLUMNS],
+                rhs=w_codes[:].bitcast(FP8X4),
+                rhs_scale=w_scales[:],
+                start=True,
+                stop=True,
+            )
 
         e_words = []
         for u in range(I // GATHER):
@@ -73,72 +88,44 @@ def tile_attend_colbert_proj_kernel(tc, emb_words, emb_scales, wp, qt, offs, out
             nc.vector.tensor_copy(words[:], pool_words[:].bitcast(U32).indirect(offsets[:, cols]))
             e_words.append(words)
 
-        for u in range(3):
-            idle = psum_a.tile([P, GATHER], F32, name="a_bank")
-            nc.tensor.matmul_mx(
-                out=idle[:],
-                lhsT=e_words[0][:, :P].bitcast(FP8X4),
-                lhsT_scale=e_top[:, :P],
-                rhs=e_words[0][:].bitcast(FP8X4),
-                rhs_scale=e_top[:, :GATHER],
-                start=True,
-                stop=True,
-            )
-
-        w_bf = keep.tile([P, PACK * PF], BF16, name="w_bf", align_bytes=64)
-        w_dst = w_bf[:].rearrange("p (t m j) -> p m j t", t=PACK, j=PACK)
-        w_src = [w[:].rearrange("p j (m t) -> p m j t", t=PACK) for w in w_raw]
-        half = P // 2
-        nc.scalar.copy(out=w_dst[:, :half], in_=w_src[0])
-        nc.vector.tensor_copy(out=w_dst[:, half:W_SPLIT], in_=w_src[1][:, : W_SPLIT - half])
-        nc.scalar.copy(out=w_dst[:, W_SPLIT:], in_=w_src[1][:, W_SPLIT - half :])
-        w_codes = keep.tile([P, PF], U32, name="w_codes", align_bytes=64)
-        w_scales = keep.tile([P, PF], U8, name="w_scales", align_bytes=64)
-        for t in range(PACK):
-            nc.vector.quantize_mx(
-                out=w_codes[:, t * P : (t + 1) * P].bitcast(FP8X4),
-                scales=w_scales[:, t * P : (t + 1) * P],
-                in_=w_bf[:, t * PF : (t + 1) * PF],
-            )
-
         q_bf = keep.tile([P, PACK * Q], BF16, name="q_bf", align_bytes=64)
         q_dst = q_bf[:].rearrange("p (h c i j) -> p c j i h", h=2, i=2, j=PACK)
         for u in range(2):
             q_src = q_raw[u][:].rearrange("p j (c i h) -> p c j i h", i=2, h=2)
-            nc.scalar.copy(out=q_dst[:, 32 * u : 32 * (u + 1)], in_=q_src)
+            nc.vector.tensor_copy(out=q_dst[:, 32 * u : 32 * (u + 1)], in_=q_src)
         q_codes = keep.tile([P, Q], U32, name="q_codes", align_bytes=64)
         q_scales = keep.tile([P, Q], U8, name="q_scales", align_bytes=64)
         nc.vector.quantize_mx(out=q_codes[:].bitcast(FP8X4), scales=q_scales[:], in_=q_bf[:])
 
         best = keep.tile([P, 2, G], F32, name="best")
-        d_all = keep.tile([P, I * PACK], BF16, name="d_all", tag="scales", align_bytes=64)
+        d_all = keep.tile([P, I * PACK], BF16, name="d_all", align_bytes=64)
+        starts = [CHUNK * sum(STAGES[:s]) for s in range(len(STAGES) + 1)]
 
-        def project(first, count):
-            for slot, n, engine in CHUNKS[first : first + count]:
+        def project(s):
+            for slot in range(starts[s], starts[s + 1], CHUNK):
                 words = e_words[slot // GATHER]
                 lo = slot % GATHER
-                bank = psum_d.tile([P, PACK, n], F32, name="d_bank")
+                bank = psum_d.tile([P, PACK, CHUNK], F32, name="d_bank")
                 for t in range(PACK):
                     nc.tensor.matmul_mx(
                         out=bank[:, t, :],
                         lhsT=w_codes[:, t * P : (t + 1) * P].bitcast(FP8X4),
                         lhsT_scale=w_scales[:, t * P : (t + 1) * P],
-                        rhs=words[:, lo : lo + n].bitcast(FP8X4),
-                        rhs_scale=e_scales[:, slot : slot + n],
+                        rhs=words[:, lo : lo + CHUNK].bitcast(FP8X4),
+                        rhs_scale=e_scales[:, slot : slot + CHUNK],
                         start=True,
                         stop=True,
                     )
-                copy = nc.vector.tensor_copy if engine == "v" else nc.scalar.copy
+                copy = nc.vector.tensor_copy if slot // CHUNK in VECTOR_CHUNKS else nc.scalar.copy
                 copy(
-                    out=d_all[:, slot * PACK : (slot + n) * PACK].rearrange("p (n t) -> p n t", t=PACK),
+                    out=d_all[:, slot * PACK : (slot + CHUNK) * PACK].rearrange("p (n t) -> p n t", t=PACK),
                     in_=bank[:].rearrange("p t n -> p n t"),
                 )
 
-        def score(first, count):
-            slot = CHUNKS[first][0]
-            n = sum(c[1] for c in CHUNKS[first : first + count])
-            d_codes = keep.tile([P, n], U32, name="d_codes%d" % first, align_bytes=64)
-            d_scales = keep.tile([P, n], U8, name="d_scales%d" % first, align_bytes=64)
+        def score(s):
+            slot, n = starts[s], starts[s + 1] - starts[s]
+            d_codes = keep.tile([P, n], U32, name="d_codes%d" % s, align_bytes=64)
+            d_scales = keep.tile([P, n], U8, name="d_scales%d" % s, align_bytes=64)
             nc.vector.quantize_mx(
                 out=d_codes[:].bitcast(FP8X4), scales=d_scales[:], in_=d_all[:, slot * PACK : (slot + n) * PACK]
             )
@@ -166,11 +153,11 @@ def tile_attend_colbert_proj_kernel(tc, emb_words, emb_scales, wp, qt, offs, out
 
         scored = []
         for s in range(AHEAD):
-            project(*STAGES[s])
-        for s, stage in enumerate(STAGES):
+            project(s)
+        for s in range(len(STAGES)):
             if s + AHEAD < len(STAGES):
-                project(*STAGES[s + AHEAD])
-            scored.append(score(*stage))
+                project(s + AHEAD)
+            scored.append(score(s))
             if s >= LAG:
                 reduce(*scored[s - LAG])
         for late in scored[len(STAGES) - LAG :]:

@@ -20,11 +20,11 @@ LIST_ROWS = 16
 QUADRANT = 32
 GATHER = 512
 CHUNK = 128
-VECTOR_CHUNKS = (3,)
-STAGES = (1, 1, 2, 2, 1, 1)
+VECTOR_CHUNKS = (4,)
+STAGES = (1, 1, 1, 1, 2, 1, 1)
 D_BANKS, A_BANKS = 4, 4
 LAG = 3
-AHEAD = 2
+AHEAD = 7
 WARM_PASSES, WARM_COLUMNS = 4, 64
 
 
@@ -32,14 +32,14 @@ def tile_attend_colbert_proj_kernel(tc, emb_words, emb_scales, wp, qt, offs, out
     nc = tc.nc
     with ExitStack() as ctx:
         keep = ctx.enter_context(tc.tile_pool(name="keep", bufs=1))
+        reused = ctx.enter_context(tc.tile_pool(name="reused", bufs=1))
         psum_d = ctx.enter_context(tc.psum_pool(name="psum_d", bufs=D_BANKS))
         psum_a = ctx.enter_context(tc.psum_pool(name="psum_a", bufs=A_BANKS))
 
         offsets = keep.tile([P, I // LIST_ROWS], U16, name="offsets")
         pool_scales = keep.tile([P, T], U8, name="pool_scales", align_bytes=64)
         pool_words = keep.tile([P, T], I32, name="pool_words", align_bytes=64)
-        w_raw = keep.tile([P, PACK, PF], F32, name="w_raw")
-        q_raw = [keep.tile([P, PACK, Q // 2], F32, name="q_raw%d" % u) for u in range(2)]
+        w_raw = reused.tile([P, PACK, PF], F32, name="w_raw", offset=0)
         e_scales = keep.tile([P, I], U8, name="e_scales", align_bytes=64)
 
         nc.vector.memset(pool_scales[:].bitcast(I32), 0)
@@ -53,18 +53,19 @@ def tile_attend_colbert_proj_kernel(tc, emb_words, emb_scales, wp, qt, offs, out
         e_spread = keep.tile([P, I], U8, name="e_spread", align_bytes=64)
         nc.vector.tensor_copy(e_spread[:], pool_scales[:].indirect(offsets[:]))
         for r in range(4):
-            nc.sync.dma_start(
+            nc.scalar.dma_start(
                 out=e_scales[r:P:QUADRANT, :].bitcast(I32), in_=e_spread[32 + 4 * r : 96 : 16, :].bitcast(I32)
             )
-        q_rows = qt.rearrange("(p j) c -> p j c", j=PACK)
-        for u in range(2):
-            nc.sync.dma_start(out=q_raw[u][:], in_=q_rows[:, :, u * Q // 2 : (u + 1) * Q // 2])
 
         w_bf = keep.tile([P, PACK * PF], BF16, name="w_bf", align_bytes=64)
         nc.scalar.copy(
             out=w_bf[:].rearrange("p (t m j) -> p m j t", t=PACK, j=PACK),
             in_=w_raw[:].rearrange("p j (m t) -> p m j t", t=PACK),
         )
+        q_raw = [reused.tile([P, PACK, Q // 2], F32, name="q_raw%d" % u, offset=u * 2048) for u in range(2)]
+        q_rows = qt.rearrange("(p j) c -> p j c", j=PACK)
+        for u in range(2):
+            nc.sync.dma_start(out=q_raw[u][:], in_=q_rows[:, :, u * Q // 2 : (u + 1) * Q // 2])
         w_codes = keep.tile([P, PF], U32, name="w_codes", align_bytes=64)
         w_scales = keep.tile([P, PF], U8, name="w_scales", align_bytes=64)
         nc.vector.quantize_mx(out=w_codes[:].bitcast(FP8X4), scales=w_scales[:], in_=w_bf[:])

@@ -23,8 +23,9 @@ CHUNK = 128
 VECTOR_CHUNKS = (4,)
 STAGES = (1, 1, 1, 1, 2, 1, 1)
 D_BANKS, A_BANKS = 4, 4
-LAG = 3
-AHEAD = 7
+LAG = 2
+AHEAD = 4
+SYNC_MOVES = 1
 WARM_PASSES, WARM_COLUMNS = 4, 64
 
 
@@ -53,7 +54,8 @@ def tile_attend_colbert_proj_kernel(tc, emb_words, emb_scales, wp, qt, offs, out
         e_spread = keep.tile([P, I], U8, name="e_spread", align_bytes=64)
         nc.vector.tensor_copy(e_spread[:], pool_scales[:].indirect(offsets[:]))
         for r in range(4):
-            nc.scalar.dma_start(
+            queue = nc.sync if r < SYNC_MOVES else nc.scalar
+            queue.dma_start(
                 out=e_scales[r:P:QUADRANT, :].bitcast(I32), in_=e_spread[32 + 4 * r : 96 : 16, :].bitcast(I32)
             )
 
@@ -153,12 +155,12 @@ def tile_attend_colbert_proj_kernel(tc, emb_words, emb_scales, wp, qt, offs, out
             )
 
         scored = []
-        for s in range(AHEAD):
+        for s in range(AHEAD + 1):
             project(s)
         for s in range(len(STAGES)):
-            if s + AHEAD < len(STAGES):
-                project(s + AHEAD)
             scored.append(score(s))
+            if s > 0 and s + AHEAD < len(STAGES):
+                project(s + AHEAD)
             if s >= LAG:
                 reduce(*scored[s - LAG])
         for late in scored[len(STAGES) - LAG :]:

@@ -20,11 +20,13 @@ LIST_ROWS = 16
 QUADRANT = 32
 GATHER = 512
 CHUNK = 128
+BANK_BYTES = 2048
 VECTOR_CHUNKS = (4,)
 STAGES = (1, 1, 1, 1, 2, 1, 1)
-D_BANKS, A_BANKS = 4, 4
 LAG = 2
-AHEAD = 4
+AHEAD = 7
+RING = 3
+W_SPLIT = 80
 SYNC_MOVES = 1
 WARM_PASSES, WARM_COLUMNS = 4, 64
 
@@ -34,13 +36,13 @@ def tile_attend_colbert_proj_kernel(tc, emb_words, emb_scales, wp, qt, offs, out
     with ExitStack() as ctx:
         keep = ctx.enter_context(tc.tile_pool(name="keep", bufs=1))
         reused = ctx.enter_context(tc.tile_pool(name="reused", bufs=1))
-        psum_d = ctx.enter_context(tc.psum_pool(name="psum_d", bufs=D_BANKS))
-        psum_a = ctx.enter_context(tc.psum_pool(name="psum_a", bufs=A_BANKS))
+        ring = ctx.enter_context(tc.tile_pool(name="ring", bufs=RING))
+        psum = ctx.enter_context(tc.psum_pool(name="psum", bufs=1))
 
         offsets = keep.tile([P, I // LIST_ROWS], U16, name="offsets")
-        pool_scales = keep.tile([P, T], U8, name="pool_scales", align_bytes=64)
+        pool_scales = reused.tile([P, T], U8, name="pool_scales", offset=0, align_bytes=64)
         pool_words = keep.tile([P, T], I32, name="pool_words", align_bytes=64)
-        w_raw = reused.tile([P, PACK, PF], F32, name="w_raw", offset=0)
+        w_raw = keep.tile([P, PACK, PF], F32, name="w_raw")
         e_scales = keep.tile([P, I], U8, name="e_scales", align_bytes=64)
 
         nc.vector.memset(pool_scales[:].bitcast(I32), 0)
@@ -58,22 +60,24 @@ def tile_attend_colbert_proj_kernel(tc, emb_words, emb_scales, wp, qt, offs, out
             queue.dma_start(
                 out=e_scales[r:P:QUADRANT, :].bitcast(I32), in_=e_spread[32 + 4 * r : 96 : 16, :].bitcast(I32)
             )
+        q_rows = qt.rearrange("(p j) c -> p j c", j=PACK)
+        q_raw = []
+        for u in range(2):
+            half = reused.tile([P, PACK, Q // 2], F32, name="q_raw%d" % u, offset=u * T // 2, align_bytes=64)
+            nc.scalar.dma_start(out=half[:], in_=q_rows[:, :, u * Q // 2 : (u + 1) * Q // 2])
+            q_raw.append(half)
 
         w_bf = keep.tile([P, PACK * PF], BF16, name="w_bf", align_bytes=64)
-        nc.scalar.copy(
-            out=w_bf[:].rearrange("p (t m j) -> p m j t", t=PACK, j=PACK),
-            in_=w_raw[:].rearrange("p j (m t) -> p m j t", t=PACK),
-        )
-        q_raw = [reused.tile([P, PACK, Q // 2], F32, name="q_raw%d" % u, offset=u * 2048) for u in range(2)]
-        q_rows = qt.rearrange("(p j) c -> p j c", j=PACK)
-        for u in range(2):
-            nc.sync.dma_start(out=q_raw[u][:], in_=q_rows[:, :, u * Q // 2 : (u + 1) * Q // 2])
+        w_dst = w_bf[:].rearrange("p (t m j) -> p m j t", t=PACK, j=PACK)
+        w_src = w_raw[:].rearrange("p j (m t) -> p m j t", t=PACK)
+        nc.scalar.copy(out=w_dst[:, :W_SPLIT], in_=w_src[:, :W_SPLIT])
+        nc.vector.tensor_copy(out=w_dst[:, W_SPLIT:], in_=w_src[:, W_SPLIT:])
         w_codes = keep.tile([P, PF], U32, name="w_codes", align_bytes=64)
         w_scales = keep.tile([P, PF], U8, name="w_scales", align_bytes=64)
         nc.vector.quantize_mx(out=w_codes[:].bitcast(FP8X4), scales=w_scales[:], in_=w_bf[:])
 
         for u in range(WARM_PASSES):
-            idle = psum_a.tile([P, PF], F32, name="a_bank")
+            idle = psum.tile([P, PF], F32, name="idle%d" % u, offset=(4 + u) * BANK_BYTES)
             nc.tensor.matmul_mx(
                 out=idle[:WARM_COLUMNS, :],
                 lhsT=w_codes[:, :WARM_COLUMNS].bitcast(FP8X4),
@@ -92,47 +96,55 @@ def tile_attend_colbert_proj_kernel(tc, emb_words, emb_scales, wp, qt, offs, out
             e_words.append(words)
 
         q_bf = keep.tile([P, PACK * Q], BF16, name="q_bf", align_bytes=64)
-        q_dst = q_bf[:].rearrange("p (h c i j) -> p c j i h", h=2, i=2, j=PACK)
-        for u in range(2):
-            q_src = q_raw[u][:].rearrange("p j (c i h) -> p c j i h", i=2, h=2)
-            nc.vector.tensor_copy(out=q_dst[:, 32 * u : 32 * (u + 1)], in_=q_src)
         q_codes = keep.tile([P, Q], U32, name="q_codes", align_bytes=64)
         q_scales = keep.tile([P, Q], U8, name="q_scales", align_bytes=64)
-        nc.vector.quantize_mx(out=q_codes[:].bitcast(FP8X4), scales=q_scales[:], in_=q_bf[:])
+        q_dst = q_bf[:].rearrange("p (h c i j) -> p c j i h", h=2, i=2, j=PACK)
+        q_src = [half[:].rearrange("p j (c i h) -> p c j i h", i=2, h=2) for half in q_raw]
+        nc.vector.tensor_copy(out=q_dst[:, :32], in_=q_src[0])
+        for h in range(2):
+            nc.vector.tensor_copy(out=q_dst[:, 32:, :, :, h], in_=q_src[1][:, :, :, :, h])
+        for h in range(2):
+            nc.vector.quantize_mx(
+                out=q_codes[:, h * P : (h + 1) * P].bitcast(FP8X4),
+                scales=q_scales[:, h * P : (h + 1) * P],
+                in_=q_bf[:, h * PACK * P : (h + 1) * PACK * P],
+            )
 
         best = keep.tile([P, 2, G], F32, name="best")
         d_all = keep.tile([P, I * PACK], BF16, name="d_all", align_bytes=64)
-        starts = [CHUNK * sum(STAGES[:s]) for s in range(len(STAGES) + 1)]
+        starts = [sum(STAGES[:s]) for s in range(len(STAGES) + 1)]
+        made = []
 
-        def project(s):
-            for slot in range(starts[s], starts[s + 1], CHUNK):
-                words = e_words[slot // GATHER]
-                lo = slot % GATHER
-                bank = psum_d.tile([P, PACK, CHUNK], F32, name="d_bank")
-                for t in range(PACK):
-                    nc.tensor.matmul_mx(
-                        out=bank[:, t, :],
-                        lhsT=w_codes[:, t * P : (t + 1) * P].bitcast(FP8X4),
-                        lhsT_scale=w_scales[:, t * P : (t + 1) * P],
-                        rhs=words[:, lo : lo + CHUNK].bitcast(FP8X4),
-                        rhs_scale=e_scales[:, slot : slot + CHUNK],
-                        start=True,
-                        stop=True,
-                    )
-                copy = nc.vector.tensor_copy if slot // CHUNK in VECTOR_CHUNKS else nc.scalar.copy
-                copy(
-                    out=d_all[:, slot * PACK : (slot + CHUNK) * PACK].rearrange("p (n t) -> p n t", t=PACK),
-                    in_=bank[:].rearrange("p t n -> p n t"),
+        def project(chunk):
+            slot = chunk * CHUNK
+            words = e_words[slot // GATHER]
+            lo = slot % GATHER
+            bank = psum.tile([P, PACK, CHUNK], F32, name="d_bank%d" % chunk, offset=chunk * BANK_BYTES)
+            for t in range(PACK):
+                nc.tensor.matmul_mx(
+                    out=bank[:, t, :],
+                    lhsT=w_codes[:, t * P : (t + 1) * P].bitcast(FP8X4),
+                    lhsT_scale=w_scales[:, t * P : (t + 1) * P],
+                    rhs=words[:, lo : lo + CHUNK].bitcast(FP8X4),
+                    rhs_scale=e_scales[:, slot : slot + CHUNK],
+                    start=True,
+                    stop=True,
                 )
+            copy = nc.vector.tensor_copy if chunk in VECTOR_CHUNKS else nc.scalar.copy
+            copy(
+                out=d_all[:, slot * PACK : (slot + CHUNK) * PACK].rearrange("p (n t) -> p n t", t=PACK),
+                in_=bank[:].rearrange("p t n -> p n t"),
+            )
 
         def score(s):
-            slot, n = starts[s], starts[s + 1] - starts[s]
-            d_codes = keep.tile([P, n], U32, name="d_codes%d" % s, align_bytes=64)
-            d_scales = keep.tile([P, n], U8, name="d_scales%d" % s, align_bytes=64)
+            slot, n = starts[s] * CHUNK, STAGES[s] * CHUNK
+            d_codes = ring.tile([P, n], U32, name="d_codes", align_bytes=64)
+            d_scales = ring.tile([P, n], U8, name="d_scales", align_bytes=64)
             nc.vector.quantize_mx(
                 out=d_codes[:].bitcast(FP8X4), scales=d_scales[:], in_=d_all[:, slot * PACK : (slot + n) * PACK]
             )
-            bank = psum_a.tile([P, 2, n], F32, name="a_bank")
+            made.append(d_codes)
+            bank = psum.tile([P, 2, n], F32, name="a_bank%d" % s, offset=s * BANK_BYTES)
             for h in range(2):
                 nc.tensor.matmul_mx(
                     out=bank[:, h, :],
@@ -155,12 +167,12 @@ def tile_attend_colbert_proj_kernel(tc, emb_words, emb_scales, wp, qt, offs, out
             )
 
         scored = []
-        for s in range(AHEAD + 1):
-            project(s)
+        for chunk in range(AHEAD):
+            project(chunk)
         for s in range(len(STAGES)):
             scored.append(score(s))
-            if s > 0 and s + AHEAD < len(STAGES):
-                project(s + AHEAD)
+            if s >= 0 and AHEAD + s - 0 < I // CHUNK:
+                project(AHEAD + s - 0)
             if s >= LAG:
                 reduce(*scored[s - LAG])
         for late in scored[len(STAGES) - LAG :]:

@@ -21,11 +21,11 @@ QUADRANT = 32
 GATHER = 512
 CHUNK = 128
 BANK_BYTES = 2048
-VECTOR_CHUNKS = (4,)
-STAGES = (1, 1, 1, 1, 2, 1, 1)
-LAG = 2
+VECTOR_SHARES = ((128, 256),)
+STAGES = (128, 128, 128, 128, 128, 128, 128, 64, 64)
+LAG = 3
 AHEAD = 7
-RING = 3
+RING = 4
 W_SPLIT = 80
 SYNC_MOVES = 1
 WARM_PASSES, WARM_COLUMNS = 4, 64
@@ -36,12 +36,13 @@ def tile_attend_colbert_proj_kernel(tc, emb_words, emb_scales, wp, qt, offs, out
     with ExitStack() as ctx:
         keep = ctx.enter_context(tc.tile_pool(name="keep", bufs=1))
         reused = ctx.enter_context(tc.tile_pool(name="reused", bufs=1))
+        late = ctx.enter_context(tc.tile_pool(name="late", bufs=1))
         ring = ctx.enter_context(tc.tile_pool(name="ring", bufs=RING))
         psum = ctx.enter_context(tc.psum_pool(name="psum", bufs=1))
 
         offsets = keep.tile([P, I // LIST_ROWS], U16, name="offsets")
         pool_scales = reused.tile([P, T], U8, name="pool_scales", offset=0, align_bytes=64)
-        pool_words = keep.tile([P, T], I32, name="pool_words", align_bytes=64)
+        pool_words = late.tile([P, T], I32, name="pool_words", offset=0, align_bytes=64)
         w_raw = keep.tile([P, PACK, PF], F32, name="w_raw")
         e_scales = keep.tile([P, I], U8, name="e_scales", align_bytes=64)
 
@@ -96,24 +97,19 @@ def tile_attend_colbert_proj_kernel(tc, emb_words, emb_scales, wp, qt, offs, out
             e_words.append(words)
 
         q_bf = keep.tile([P, PACK * Q], BF16, name="q_bf", align_bytes=64)
-        q_codes = keep.tile([P, Q], U32, name="q_codes", align_bytes=64)
+        q_codes = late.tile([P, Q], U32, name="q_codes", offset=0, align_bytes=64)
         q_scales = keep.tile([P, Q], U8, name="q_scales", align_bytes=64)
-        q_dst = q_bf[:].rearrange("p (h c i j) -> p c j i h", h=2, i=2, j=PACK)
-        q_src = [half[:].rearrange("p j (c i h) -> p c j i h", i=2, h=2) for half in q_raw]
-        nc.vector.tensor_copy(out=q_dst[:, :32], in_=q_src[0])
-        for h in range(2):
-            nc.vector.tensor_copy(out=q_dst[:, 32:, :, :, h], in_=q_src[1][:, :, :, :, h])
-        for h in range(2):
-            nc.vector.quantize_mx(
-                out=q_codes[:, h * P : (h + 1) * P].bitcast(FP8X4),
-                scales=q_scales[:, h * P : (h + 1) * P],
-                in_=q_bf[:, h * PACK * P : (h + 1) * PACK * P],
+        q_dst = q_bf[:].rearrange("p (h m j) -> p h m j", h=2, j=PACK)
+        for u in range(2):
+            src = q_raw[u][:].rearrange("p j (m h) -> p h m j", h=2)
+            nc.gpsimd.tensor_scalar(
+                q_dst[:, :, u * 64 : (u + 1) * 64, :], src, 1.0, 0.0, mybir.AluOpType.mult, mybir.AluOpType.add
             )
+        nc.vector.quantize_mx(out=q_codes[:].bitcast(FP8X4), scales=q_scales[:], in_=q_bf[:])
 
         best = keep.tile([P, 2, G], F32, name="best")
         d_all = keep.tile([P, I * PACK], BF16, name="d_all", align_bytes=64)
         starts = [sum(STAGES[:s]) for s in range(len(STAGES) + 1)]
-        made = []
 
         def project(chunk):
             slot = chunk * CHUNK
@@ -130,21 +126,23 @@ def tile_attend_colbert_proj_kernel(tc, emb_words, emb_scales, wp, qt, offs, out
                     start=True,
                     stop=True,
                 )
-            copy = nc.vector.tensor_copy if chunk in VECTOR_CHUNKS else nc.scalar.copy
-            copy(
-                out=d_all[:, slot * PACK : (slot + CHUNK) * PACK].rearrange("p (n t) -> p n t", t=PACK),
-                in_=bank[:].rearrange("p t n -> p n t"),
-            )
+            ends = set(starts + [c for share in VECTOR_SHARES for c in share])
+            cuts = sorted(c for c in ends if slot <= c <= slot + CHUNK)
+            for a, b in zip(cuts[:-1], cuts[1:]):
+                copy = nc.vector.tensor_copy if (a, b) in VECTOR_SHARES else nc.scalar.copy
+                copy(
+                    out=d_all[:, a * PACK : b * PACK].rearrange("p (n t) -> p n t", t=PACK),
+                    in_=bank[:, :, a - slot : b - slot].rearrange("p t n -> p n t"),
+                )
 
         def score(s):
-            slot, n = starts[s] * CHUNK, STAGES[s] * CHUNK
+            slot, n = starts[s], STAGES[s]
             d_codes = ring.tile([P, n], U32, name="d_codes", align_bytes=64)
             d_scales = ring.tile([P, n], U8, name="d_scales", align_bytes=64)
             nc.vector.quantize_mx(
                 out=d_codes[:].bitcast(FP8X4), scales=d_scales[:], in_=d_all[:, slot * PACK : (slot + n) * PACK]
             )
-            made.append(d_codes)
-            bank = psum.tile([P, 2, n], F32, name="a_bank%d" % s, offset=s * BANK_BYTES)
+            bank = psum.tile([P, 2, n], F32, name="a_bank%d" % s, offset=(s % 8) * BANK_BYTES)
             for h in range(2):
                 nc.tensor.matmul_mx(
                     out=bank[:, h, :],
@@ -171,11 +169,11 @@ def tile_attend_colbert_proj_kernel(tc, emb_words, emb_scales, wp, qt, offs, out
             project(chunk)
         for s in range(len(STAGES)):
             scored.append(score(s))
-            if s >= 0 and AHEAD + s - 0 < I // CHUNK:
-                project(AHEAD + s - 0)
+            if AHEAD + s < I // CHUNK:
+                project(AHEAD + s)
             if s >= LAG:
                 reduce(*scored[s - LAG])
-        for late in scored[len(STAGES) - LAG :]:
-            reduce(*late)
+        for last in scored[len(STAGES) - LAG :]:
+            reduce(*last)
 
         nc.sync.dma_start(out=out.rearrange("(m h) g -> m (h g)", h=2), in_=best[:].rearrange("p h g -> p (h g)"))

@@ -21,7 +21,8 @@ QUADRANT = 32
 GATHER = 512
 CHUNK = 128
 BANK_BYTES = 2048
-VECTOR_SHARES = ((128, 256),)
+VECTOR_SHARES = ((512, 640),)
+Q_SPLIT = 24
 STAGES = (128, 128, 128, 128, 128, 128, 128, 64, 64)
 LAG = 3
 AHEAD = 7
@@ -99,12 +100,11 @@ def tile_attend_colbert_proj_kernel(tc, emb_words, emb_scales, wp, qt, offs, out
         q_bf = keep.tile([P, PACK * Q], BF16, name="q_bf", align_bytes=64)
         q_codes = late.tile([P, Q], U32, name="q_codes", offset=0, align_bytes=64)
         q_scales = keep.tile([P, Q], U8, name="q_scales", align_bytes=64)
-        q_dst = q_bf[:].rearrange("p (h m j) -> p h m j", h=2, j=PACK)
-        for u in range(2):
-            src = q_raw[u][:].rearrange("p j (m h) -> p h m j", h=2)
-            nc.gpsimd.tensor_scalar(
-                q_dst[:, :, u * 64 : (u + 1) * 64, :], src, 1.0, 0.0, mybir.AluOpType.mult, mybir.AluOpType.add
-            )
+        q_dst = q_bf[:].rearrange("p (h c i j) -> p c j i h", h=2, i=2, j=PACK)
+        q_src = [half[:].rearrange("p j (c i h) -> p c j i h", i=2, h=2) for half in q_raw]
+        nc.scalar.copy(out=q_dst[:, :Q_SPLIT], in_=q_src[0][:, :Q_SPLIT])
+        nc.vector.tensor_copy(out=q_dst[:, Q_SPLIT:32], in_=q_src[0][:, Q_SPLIT:])
+        nc.vector.tensor_copy(out=q_dst[:, 32:], in_=q_src[1])
         nc.vector.quantize_mx(out=q_codes[:].bitcast(FP8X4), scales=q_scales[:], in_=q_bf[:])
 
         best = keep.tile([P, 2, G], F32, name="best")
@@ -126,7 +126,7 @@ def tile_attend_colbert_proj_kernel(tc, emb_words, emb_scales, wp, qt, offs, out
                     start=True,
                     stop=True,
                 )
-            ends = set(starts + [c for share in VECTOR_SHARES for c in share])
+            ends = set(starts + [slot, slot + CHUNK] + [c for share in VECTOR_SHARES for c in share])
             cuts = sorted(c for c in ends if slot <= c <= slot + CHUNK)
             for a, b in zip(cuts[:-1], cuts[1:]):
                 copy = nc.vector.tensor_copy if (a, b) in VECTOR_SHARES else nc.scalar.copy

@@ -22,7 +22,6 @@ GATHER = 512
 CHUNK = 128
 BANK_BYTES = 2048
 VECTOR_SHARES = ((512, 640),)
-Q_SPLIT = 24
 STAGES = (128, 128, 128, 128, 128, 128, 128, 64, 64)
 LAG = 3
 AHEAD = 7
@@ -102,10 +101,15 @@ def tile_attend_colbert_proj_kernel(tc, emb_words, emb_scales, wp, qt, offs, out
         q_scales = keep.tile([P, Q], U8, name="q_scales", align_bytes=64)
         q_dst = q_bf[:].rearrange("p (h c i j) -> p c j i h", h=2, i=2, j=PACK)
         q_src = [half[:].rearrange("p j (c i h) -> p c j i h", i=2, h=2) for half in q_raw]
-        nc.scalar.copy(out=q_dst[:, :Q_SPLIT], in_=q_src[0][:, :Q_SPLIT])
-        nc.vector.tensor_copy(out=q_dst[:, Q_SPLIT:32], in_=q_src[0][:, Q_SPLIT:])
-        nc.vector.tensor_copy(out=q_dst[:, 32:], in_=q_src[1])
-        nc.vector.quantize_mx(out=q_codes[:].bitcast(FP8X4), scales=q_scales[:], in_=q_bf[:])
+        nc.scalar.copy(out=q_dst[:, :32], in_=q_src[0])
+        for h in range(2):
+            nc.vector.tensor_copy(out=q_dst[:, 32:, :, :, h], in_=q_src[1][:, :, :, :, h])
+        for h in range(2):
+            nc.vector.quantize_mx(
+                out=q_codes[:, h * P : (h + 1) * P].bitcast(FP8X4),
+                scales=q_scales[:, h * P : (h + 1) * P],
+                in_=q_bf[:, h * PACK * P : (h + 1) * PACK * P],
+            )
 
         best = keep.tile([P, 2, G], F32, name="best")
         d_all = keep.tile([P, I * PACK], BF16, name="d_all", align_bytes=64)

@@ -23,9 +23,10 @@ CHUNK = 128
 BANK_BYTES = 2048
 VECTOR_SHARES = ((512, 640),)
 STAGES = (128, 128, 128, 128, 128, 128, 128, 64, 64)
+ORDER = (0, 1, 2, 4, 3, 5, 6, 7, 8)
 LAG = 3
 AHEAD = 7
-RING = 4
+RING = 5
 W_SPLIT = 80
 SYNC_MOVES = 1
 WARM_PASSES, WARM_COLUMNS = 4, 64
@@ -172,7 +173,7 @@ def tile_attend_colbert_proj_kernel(tc, emb_words, emb_scales, wp, qt, offs, out
         for chunk in range(AHEAD):
             project(chunk)
         for s in range(len(STAGES)):
-            scored.append(score(s))
+            scored.append(score(ORDER[s]))
             if AHEAD + s < I // CHUNK:
                 project(AHEAD + s)
             if s >= LAG:

@@ -18,18 +18,18 @@ PACK = 4
 RUN = I // G
 LIST_ROWS = 16
 QUADRANT = 32
-GATHER = 512
-CHUNK = 128
 BANK_BYTES = 2048
-VECTOR_SHARES = ((512, 640),)
+GATHERS = (256, 256, 512,)
+CHUNK = 128
+VECTOR_SHARE = (384, 512)
 STAGES = (128, 128, 128, 128, 128, 128, 128, 64, 64)
-ORDER = (0, 1, 2, 4, 3, 5, 6, 7, 8)
-LAG = 3
-AHEAD = 7
-RING = 5
-W_SPLIT = 80
-SYNC_MOVES = 1
-WARM_PASSES, WARM_COLUMNS = 4, 64
+CHUNK_BANKS = (0, 1, 2, 3, 4, 5, 6, 7)
+SCORE_BANKS = (0, 1, 2, 3, 4, 5, 6, 7, 0)
+WORD_PLACES = (512, 2048, 3072)
+EARLY = 48
+RING = 4
+W_FIRST = 320
+WARM_PASSES, WARM_COLUMNS = 4, 32
 
 
 def tile_attend_colbert_proj_kernel(tc, emb_words, emb_scales, wp, qt, offs, out):
@@ -37,6 +37,8 @@ def tile_attend_colbert_proj_kernel(tc, emb_words, emb_scales, wp, qt, offs, out
     with ExitStack() as ctx:
         keep = ctx.enter_context(tc.tile_pool(name="keep", bufs=1))
         reused = ctx.enter_context(tc.tile_pool(name="reused", bufs=1))
+        shared = ctx.enter_context(tc.tile_pool(name="shared", bufs=1))
+        gathered = ctx.enter_context(tc.tile_pool(name="gathered", bufs=1))
         late = ctx.enter_context(tc.tile_pool(name="late", bufs=1))
         ring = ctx.enter_context(tc.tile_pool(name="ring", bufs=RING))
         psum = ctx.enter_context(tc.psum_pool(name="psum", bufs=1))
@@ -44,39 +46,41 @@ def tile_attend_colbert_proj_kernel(tc, emb_words, emb_scales, wp, qt, offs, out
         offsets = keep.tile([P, I // LIST_ROWS], U16, name="offsets")
         pool_scales = reused.tile([P, T], U8, name="pool_scales", offset=0, align_bytes=64)
         pool_words = late.tile([P, T], I32, name="pool_words", offset=0, align_bytes=64)
-        w_raw = keep.tile([P, PACK, PF], F32, name="w_raw")
+        w_first = keep.tile([P, PACK, W_FIRST], F32, name="w_first")
+        w_rest = keep.tile([P, PACK, PF - W_FIRST], F32, name="w_rest")
         e_scales = keep.tile([P, I], U8, name="e_scales", align_bytes=64)
 
         nc.vector.memset(pool_scales[:].bitcast(I32), 0)
         nc.vector.memset(e_scales[:].bitcast(I32), 0)
 
-        nc.sync.dma_start(out=w_raw[:], in_=wp.rearrange("(p j) c -> p j c", j=PACK))
+        w_rows = wp.rearrange("(p j) c -> p j c", j=PACK)
+        nc.sync.dma_start(out=w_first[:], in_=w_rows[:, :, :W_FIRST])
         nc.sync.dma_start(offsets[:], offs)
         nc.sync.dma_start(out=pool_scales[32:96:4, :].bitcast(I32), in_=emb_scales[0].bitcast(I32))
+        nc.sync.dma_start(out=w_rest[:], in_=w_rows[:, :, W_FIRST:])
         nc.sync.dma_start(out=pool_words[:], in_=emb_words[0].rearrange("p n t -> p (n t)").bitcast(I32))
 
         e_spread = keep.tile([P, I], U8, name="e_spread", align_bytes=64)
         nc.vector.tensor_copy(e_spread[:], pool_scales[:].indirect(offsets[:]))
         for r in range(4):
-            queue = nc.sync if r < SYNC_MOVES else nc.scalar
-            queue.dma_start(
+            nc.sync.dma_start(
                 out=e_scales[r:P:QUADRANT, :].bitcast(I32), in_=e_spread[32 + 4 * r : 96 : 16, :].bitcast(I32)
             )
-        q_rows = qt.rearrange("(p j) c -> p j c", j=PACK)
-        q_raw = []
-        for u in range(2):
-            half = reused.tile([P, PACK, Q // 2], F32, name="q_raw%d" % u, offset=u * T // 2, align_bytes=64)
-            nc.scalar.dma_start(out=half[:], in_=q_rows[:, :, u * Q // 2 : (u + 1) * Q // 2])
-            q_raw.append(half)
-
-        w_bf = keep.tile([P, PACK * PF], BF16, name="w_bf", align_bytes=64)
+        w_bf = shared.tile([P, PACK * PF], BF16, name="w_bf", offset=0, align_bytes=64)
         w_dst = w_bf[:].rearrange("p (t m j) -> p m j t", t=PACK, j=PACK)
-        w_src = w_raw[:].rearrange("p j (m t) -> p m j t", t=PACK)
-        nc.scalar.copy(out=w_dst[:, :W_SPLIT], in_=w_src[:, :W_SPLIT])
-        nc.vector.tensor_copy(out=w_dst[:, W_SPLIT:], in_=w_src[:, W_SPLIT:])
+        done = W_FIRST // PACK
+        nc.scalar.copy(out=w_dst[:, :done], in_=w_first[:].rearrange("p j (m t) -> p m j t", t=PACK))
+        nc.scalar.copy(out=w_dst[:, done:], in_=w_rest[:].rearrange("p j (m t) -> p m j t", t=PACK))
         w_codes = keep.tile([P, PF], U32, name="w_codes", align_bytes=64)
         w_scales = keep.tile([P, PF], U8, name="w_scales", align_bytes=64)
         nc.vector.quantize_mx(out=w_codes[:].bitcast(FP8X4), scales=w_scales[:], in_=w_bf[:])
+
+        q_rows = qt.rearrange("(p j) c -> p j c", j=PACK)
+        q_raw = []
+        for h in range(2):
+            half = shared.tile([P, PACK, P], F32, name="q_raw%d" % h, offset=h * T // 2, align_bytes=64)
+            nc.scalar.dma_start(out=half[:], in_=q_rows[:, :, h * P : (h + 1) * P])
+            q_raw.append(half)
 
         for u in range(WARM_PASSES):
             idle = psum.tile([P, PF], F32, name="idle%d" % u, offset=(4 + u) * BANK_BYTES)
@@ -91,36 +95,29 @@ def tile_attend_colbert_proj_kernel(tc, emb_words, emb_scales, wp, qt, offs, out
             )
 
         e_words = []
-        for u in range(I // GATHER):
-            words = keep.tile([P, GATHER], U32, name="e_words%d" % u, align_bytes=64)
-            cols = slice(u * GATHER // LIST_ROWS, (u + 1) * GATHER // LIST_ROWS)
+        first = 0
+        for u, n in enumerate(GATHERS):
+            words = gathered.tile([P, n], U32, name="e_words%d" % u, offset=WORD_PLACES[u], align_bytes=64)
+            cols = slice(first // LIST_ROWS, (first + n) // LIST_ROWS)
             nc.vector.tensor_copy(words[:], pool_words[:].bitcast(U32).indirect(offsets[:, cols]))
-            e_words.append(words)
+            e_words.append((first, n, words))
+            first = first + n
 
-        q_bf = keep.tile([P, PACK * Q], BF16, name="q_bf", align_bytes=64)
-        q_codes = late.tile([P, Q], U32, name="q_codes", offset=0, align_bytes=64)
+        q_codes = gathered.tile([P, Q], U32, name="q_codes", offset=1024, align_bytes=64)
         q_scales = keep.tile([P, Q], U8, name="q_scales", align_bytes=64)
-        q_dst = q_bf[:].rearrange("p (h c i j) -> p c j i h", h=2, i=2, j=PACK)
-        q_src = [half[:].rearrange("p j (c i h) -> p c j i h", i=2, h=2) for half in q_raw]
-        nc.scalar.copy(out=q_dst[:, :32], in_=q_src[0])
-        for h in range(2):
-            nc.vector.tensor_copy(out=q_dst[:, 32:, :, :, h], in_=q_src[1][:, :, :, :, h])
-        for h in range(2):
-            nc.vector.quantize_mx(
-                out=q_codes[:, h * P : (h + 1) * P].bitcast(FP8X4),
-                scales=q_scales[:, h * P : (h + 1) * P],
-                in_=q_bf[:, h * PACK * P : (h + 1) * PACK * P],
-            )
-
+        q_bf = [
+            keep.tile([P, PACK * P], BF16, name="q_bf0", align_bytes=64),
+            gathered.tile([P, PACK * P], BF16, name="q_bf1", offset=0, align_bytes=64),
+        ]
         best = keep.tile([P, 2, G], F32, name="best")
         d_all = keep.tile([P, I * PACK], BF16, name="d_all", align_bytes=64)
         starts = [sum(STAGES[:s]) for s in range(len(STAGES) + 1)]
+        scored = {}
 
-        def project(chunk):
-            slot = chunk * CHUNK
-            words = e_words[slot // GATHER]
-            lo = slot % GATHER
-            bank = psum.tile([P, PACK, CHUNK], F32, name="d_bank%d" % chunk, offset=chunk * BANK_BYTES)
+        def project(c):
+            slot = c * CHUNK
+            lo, words = [(slot - a, w) for a, m, w in e_words if a <= slot < a + m][0]
+            bank = psum.tile([P, PACK, CHUNK], F32, name="d_bank%d" % c, offset=CHUNK_BANKS[c] * BANK_BYTES)
             for t in range(PACK):
                 nc.tensor.matmul_mx(
                     out=bank[:, t, :],
@@ -131,10 +128,9 @@ def tile_attend_colbert_proj_kernel(tc, emb_words, emb_scales, wp, qt, offs, out
                     start=True,
                     stop=True,
                 )
-            ends = set(starts + [slot, slot + CHUNK] + [c for share in VECTOR_SHARES for c in share])
-            cuts = sorted(c for c in ends if slot <= c <= slot + CHUNK)
+            cuts = sorted(a for a in set(starts + list(VECTOR_SHARE)) if slot <= a <= slot + CHUNK)
             for a, b in zip(cuts[:-1], cuts[1:]):
-                copy = nc.vector.tensor_copy if (a, b) in VECTOR_SHARES else nc.scalar.copy
+                copy = nc.vector.tensor_copy if (a, b) == VECTOR_SHARE else nc.scalar.copy
                 copy(
                     out=d_all[:, a * PACK : b * PACK].rearrange("p (n t) -> p n t", t=PACK),
                     in_=bank[:, :, a - slot : b - slot].rearrange("p t n -> p n t"),
@@ -147,7 +143,7 @@ def tile_attend_colbert_proj_kernel(tc, emb_words, emb_scales, wp, qt, offs, out
             nc.vector.quantize_mx(
                 out=d_codes[:].bitcast(FP8X4), scales=d_scales[:], in_=d_all[:, slot * PACK : (slot + n) * PACK]
             )
-            bank = psum.tile([P, 2, n], F32, name="a_bank%d" % s, offset=(s % 8) * BANK_BYTES)
+            bank = psum.tile([P, 2, n], F32, name="a_bank%d" % s, offset=SCORE_BANKS[s] * BANK_BYTES)
             for h in range(2):
                 nc.tensor.matmul_mx(
                     out=bank[:, h, :],
@@ -158,27 +154,55 @@ def tile_attend_colbert_proj_kernel(tc, emb_words, emb_scales, wp, qt, offs, out
                     start=True,
                     stop=True,
                 )
-            return bank, slot, n
+            scored[s] = bank
 
-        def reduce(bank, slot, n):
-            g0 = slot // RUN
+        def reduce(s):
+            g0 = starts[s] // RUN
             nc.vector.tensor_reduce(
-                out=best[:, :, g0 : g0 + n // RUN],
-                in_=bank[:].rearrange("p h (g s) -> p h g s", s=RUN),
+                out=best[:, :, g0 : g0 + STAGES[s] // RUN],
+                in_=scored[s][:].rearrange("p h (g s) -> p h g s", s=RUN),
                 axis=mybir.AxisListType.X,
                 op=mybir.AluOpType.max,
             )
 
-        scored = []
-        for chunk in range(AHEAD):
-            project(chunk)
-        for s in range(len(STAGES)):
-            scored.append(score(ORDER[s]))
-            if AHEAD + s < I // CHUNK:
-                project(AHEAD + s)
-            if s >= LAG:
-                reduce(*scored[s - LAG])
-        for last in scored[len(STAGES) - LAG :]:
-            reduce(*last)
+        project(0)
+        project(1)
+        for h, copy in enumerate((nc.scalar.copy, nc.vector.tensor_copy)):
+            copy(
+                out=q_bf[h][:].rearrange("p (c i j) -> p c j i", i=4, j=PACK),
+                in_=q_raw[h][:].rearrange("p j (c i) -> p c j i", i=4),
+            )
+        for h in range(2):
+            nc.vector.quantize_mx(
+                out=q_codes[:, h * P : (h + 1) * P].bitcast(FP8X4),
+                scales=q_scales[:, h * P : (h + 1) * P],
+                in_=q_bf[h][:],
+            )
+        project(2)
+        project(3)
+        project(4)
+        project(5)
+        project(6)
+        score(0)
+        project(7)
+        score(1)
+        score(2)
+        score(3)
+        reduce(0)
+        score(4)
+        reduce(1)
+        score(5)
+        reduce(2)
+        score(6)
+        reduce(3)
+        score(7)
+        reduce(4)
+        score(8)
+        reduce(5)
+        reduce(6)
+        reduce(7)
+        reduce(8)
 
-        nc.sync.dma_start(out=out.rearrange("(m h) g -> m (h g)", h=2), in_=best[:].rearrange("p h g -> p (h g)"))
+        rows = out.rearrange("(h m) g -> m h g", h=2)
+        nc.sync.dma_start(out=rows[:, :, :EARLY], in_=best[:, :, :EARLY])
+        nc.sync.dma_start(out=rows[:, :, EARLY:], in_=best[:, :, EARLY:])

from contextlib import ExitStack

import concourse.mybir as mybir

K, T, I, PF, Q, G = 512, 4096, 1024, 512, 256, 64
FLOPS = 2 * K * PF * I + 2 * PF * Q * I

F32 = mybir.dt.float32
BF16 = mybir.dt.bfloat16
I32 = mybir.dt.int32
U32 = mybir.dt.uint32
U16 = mybir.dt.uint16
U8 = mybir.dt.uint8
FP8X4 = mybir.dt.float8_e4m3fn_x4

P = 128
PACK = 4
RUN = I // G
LIST_ROWS = 16
QUADRANT = 32
BANK_BYTES = 2048
GATHERS = (256, 256, 512,)
CHUNK = 128
VECTOR_SHARE = (384, 512)
STAGES = (128, 128, 128, 128, 128, 128, 128, 64, 64)
CHUNK_BANKS = (0, 1, 2, 3, 4, 5, 6, 7)
SCORE_BANKS = (0, 1, 2, 3, 4, 5, 6, 7, 0)
WORD_PLACES = (512, 2048, 3072)
EARLY = 48
RING = 4
W_FIRST = 320
WARM_PASSES, WARM_COLUMNS = 4, 32


def tile_attend_colbert_proj_kernel(tc, emb_words, emb_scales, wp, qt, offs, out):
    nc = tc.nc
    with ExitStack() as ctx:
        keep = ctx.enter_context(tc.tile_pool(name="keep", bufs=1))
        reused = ctx.enter_context(tc.tile_pool(name="reused", bufs=1))
        shared = ctx.enter_context(tc.tile_pool(name="shared", bufs=1))
        gathered = ctx.enter_context(tc.tile_pool(name="gathered", bufs=1))
        late = ctx.enter_context(tc.tile_pool(name="late", bufs=1))
        ring = ctx.enter_context(tc.tile_pool(name="ring", bufs=RING))
        psum = ctx.enter_context(tc.psum_pool(name="psum", bufs=1))

        offsets = keep.tile([P, I // LIST_ROWS], U16, name="offsets")
        pool_scales = reused.tile([P, T], U8, name="pool_scales", offset=0, align_bytes=64)
        pool_words = late.tile([P, T], I32, name="pool_words", offset=0, align_bytes=64)
        w_first = keep.tile([P, PACK, W_FIRST], F32, name="w_first")
        w_rest = keep.tile([P, PACK, PF - W_FIRST], F32, name="w_rest")
        e_scales = keep.tile([P, I], U8, name="e_scales", align_bytes=64)

        nc.vector.memset(pool_scales[:].bitcast(I32), 0)
        nc.vector.memset(e_scales[:].bitcast(I32), 0)

        w_rows = wp.rearrange("(p j) c -> p j c", j=PACK)
        nc.sync.dma_start(out=w_first[:], in_=w_rows[:, :, :W_FIRST])
        nc.sync.dma_start(offsets[:], offs)
        nc.sync.dma_start(out=pool_scales[32:96:4, :].bitcast(I32), in_=emb_scales[0].bitcast(I32))
        nc.sync.dma_start(out=w_rest[:], in_=w_rows[:, :, W_FIRST:])
        nc.sync.dma_start(out=pool_words[:], in_=emb_words[0].rearrange("p n t -> p (n t)").bitcast(I32))

        e_spread = keep.tile([P, I], U8, name="e_spread", align_bytes=64)
        nc.vector.tensor_copy(e_spread[:], pool_scales[:].indirect(offsets[:]))
        for r in range(4):
            nc.sync.dma_start(
                out=e_scales[r:P:QUADRANT, :].bitcast(I32), in_=e_spread[32 + 4 * r : 96 : 16, :].bitcast(I32)
            )
        w_bf = shared.tile([P, PACK * PF], BF16, name="w_bf", offset=0, align_bytes=64)
        w_dst = w_bf[:].rearrange("p (t m j) -> p m j t", t=PACK, j=PACK)
        done = W_FIRST // PACK
        nc.scalar.copy(out=w_dst[:, :done], in_=w_first[:].rearrange("p j (m t) -> p m j t", t=PACK))
        nc.scalar.copy(out=w_dst[:, done:], in_=w_rest[:].rearrange("p j (m t) -> p m j t", t=PACK))
        w_codes = keep.tile([P, PF], U32, name="w_codes", align_bytes=64)
        w_scales = keep.tile([P, PF], U8, name="w_scales", align_bytes=64)
        nc.vector.quantize_mx(out=w_codes[:].bitcast(FP8X4), scales=w_scales[:], in_=w_bf[:])

        q_rows = qt.rearrange("(p j) c -> p j c", j=PACK)
        q_raw = []
        for h in range(2):
            half = shared.tile([P, PACK, P], F32, name="q_raw%d" % h, offset=h * T // 2, align_bytes=64)
            nc.scalar.dma_start(out=half[:], in_=q_rows[:, :, h * P : (h + 1) * P])
            q_raw.append(half)

        for u in range(WARM_PASSES):
            idle = psum.tile([P, PF], F32, name="idle%d" % u, offset=(4 + u) * BANK_BYTES)
            nc.tensor.matmul_mx(
                out=idle[:WARM_COLUMNS, :],
                lhsT=w_codes[:, :WARM_COLUMNS].bitcast(FP8X4),
                lhsT_scale=w_scales[:, :WARM_COLUMNS],
                rhs=w_codes[:].bitcast(FP8X4),
                rhs_scale=w_scales[:],
                start=True,
                stop=True,
            )

        e_words = []
        first = 0
        for u, n in enumerate(GATHERS):
            words = gathered.tile([P, n], U32, name="e_words%d" % u, offset=WORD_PLACES[u], align_bytes=64)
            cols = slice(first // LIST_ROWS, (first + n) // LIST_ROWS)
            nc.vector.tensor_copy(words[:], pool_words[:].bitcast(U32).indirect(offsets[:, cols]))
            e_words.append((first, n, words))
            first = first + n

        q_codes = gathered.tile([P, Q], U32, name="q_codes", offset=1024, align_bytes=64)
        q_scales = keep.tile([P, Q], U8, name="q_scales", align_bytes=64)
        q_bf = [
            keep.tile([P, PACK * P], BF16, name="q_bf0", align_bytes=64),
            gathered.tile([P, PACK * P], BF16, name="q_bf1", offset=0, align_bytes=64),
        ]
        best = keep.tile([P, 2, G], F32, name="best")
        d_all = keep.tile([P, I * PACK], BF16, name="d_all", align_bytes=64)
        starts = [sum(STAGES[:s]) for s in range(len(STAGES) + 1)]
        scored = {}

        def project(c):
            slot = c * CHUNK
            lo, words = [(slot - a, w) for a, m, w in e_words if a <= slot < a + m][0]
            bank = psum.tile([P, PACK, CHUNK], F32, name="d_bank%d" % c, offset=CHUNK_BANKS[c] * BANK_BYTES)
            for t in range(PACK):
                nc.tensor.matmul_mx(
                    out=bank[:, t, :],
                    lhsT=w_codes[:, t * P : (t + 1) * P].bitcast(FP8X4),
                    lhsT_scale=w_scales[:, t * P : (t + 1) * P],
                    rhs=words[:, lo : lo + CHUNK].bitcast(FP8X4),
                    rhs_scale=e_scales[:, slot : slot + CHUNK],
                    start=True,
                    stop=True,
                )
            cuts = sorted(a for a in set(starts + list(VECTOR_SHARE)) if slot <= a <= slot + CHUNK)
            for a, b in zip(cuts[:-1], cuts[1:]):
                copy = nc.vector.tensor_copy if (a, b) == VECTOR_SHARE else nc.scalar.copy
                copy(
                    out=d_all[:, a * PACK : b * PACK].rearrange("p (n t) -> p n t", t=PACK),
                    in_=bank[:, :, a - slot : b - slot].rearrange("p t n -> p n t"),
                )

        def score(s):
            slot, n = starts[s], STAGES[s]
            d_codes = ring.tile([P, n], U32, name="d_codes", align_bytes=64)
            d_scales = ring.tile([P, n], U8, name="d_scales", align_bytes=64)
            nc.vector.quantize_mx(
                out=d_codes[:].bitcast(FP8X4), scales=d_scales[:], in_=d_all[:, slot * PACK : (slot + n) * PACK]
            )
            bank = psum.tile([P, 2, n], F32, name="a_bank%d" % s, offset=SCORE_BANKS[s] * BANK_BYTES)
            for h in range(2):
                nc.tensor.matmul_mx(
                    out=bank[:, h, :],
                    lhsT=q_codes[:, h * P : (h + 1) * P].bitcast(FP8X4),
                    lhsT_scale=q_scales[:, h * P : (h + 1) * P],
                    rhs=d_codes[:].bitcast(FP8X4),
                    rhs_scale=d_scales[:],
                    start=True,
                    stop=True,
                )
            scored[s] = bank

        def reduce(s):
            g0 = starts[s] // RUN
            nc.vector.tensor_reduce(
                out=best[:, :, g0 : g0 + STAGES[s] // RUN],
                in_=scored[s][:].rearrange("p h (g s) -> p h g s", s=RUN),
                axis=mybir.AxisListType.X,
                op=mybir.AluOpType.max,
            )

        project(0)
        project(1)
        for h, copy in enumerate((nc.scalar.copy, nc.vector.tensor_copy)):
            copy(
                out=q_bf[h][:].rearrange("p (c i j) -> p c j i", i=4, j=PACK),
                in_=q_raw[h][:].rearrange("p j (c i) -> p c j i", i=4),
            )
        for h in range(2):
            nc.vector.quantize_mx(
                out=q_codes[:, h * P : (h + 1) * P].bitcast(FP8X4),
                scales=q_scales[:, h * P : (h + 1) * P],
                in_=q_bf[h][:],
            )
        project(2)
        project(3)
        project(4)
        project(5)
        project(6)
        score(0)
        project(7)
        score(1)
        score(2)
        score(3)
        reduce(0)
        score(4)
        reduce(1)
        score(5)
        reduce(2)
        score(6)
        reduce(3)
        score(7)
        reduce(4)
        score(8)
        reduce(5)
        reduce(6)
        reduce(7)
        reduce(8)

        rows = out.rearrange("(h m) g -> m h g", h=2)
        nc.sync.dma_start(out=rows[:, :, :EARLY], in_=best[:, :, :EARLY])
        nc.sync.dma_start(out=rows[:, :, EARLY:], in_=best[:, :, EARLY:])
